import numpy as np
import ml_dtypes


def mxq(x, axis, fmt="e4m3"):
    dtype, down = {"e4m3": (ml_dtypes.float8_e4m3fn, 7), "e5m2": (ml_dtypes.float8_e5m2, 14)}[fmt]
    v = np.moveaxis(np.asarray(x, np.float32).astype(ml_dtypes.bfloat16).astype(np.float64), axis, -1)
    blocks = v.reshape(v.shape[:-1] + (-1, 32))
    amax = np.abs(blocks).max(-1, keepdims=True)
    byte = np.maximum(np.where(amax > 0, np.frexp(amax)[1] - 1 + 127, 0) - down, 1)
    scale = np.exp2(byte - 127.0)
    codes = (blocks / scale).astype(np.float32).astype(dtype).astype(np.float64)
    return np.moveaxis((codes * scale).reshape(v.shape), -1, axis)


WIDE = False


def mx_kscale(k):
    if not WIDE:
        return np.ones(k)
    levels = np.array([10, -10, 5, -5, 0])
    if k % 512:
        return np.exp2(np.random.permutation(np.resize(levels, k // 32))).repeat(32)
    a = np.empty((k // 512, 16))
    for p in range(k // 512):
        a[p, :8] = np.random.permutation(np.resize(levels, 8))
        for g in range(8):
            far = levels[np.abs(levels - a[p, g]) >= 10]
            a[p, g + 8] = far[np.random.randint(len(far))]
    return np.exp2(a.ravel()).repeat(32)


def f64(x):
    return np.asarray(x).astype(np.float64)


def striped(idx):
    return np.tile(idx.reshape(-1, 16).T, (8, 1)).astype(np.uint16)


def unstriped(offs):
    return offs[:16].T.reshape(-1).astype(np.int64)


E2M1 = np.array([0.0, 0.5, 1.0, 1.5, 2.0, 3.0, 4.0, 6.0, -0.0, -0.5, -1.0, -1.5, -2.0, -3.0, -4.0, -6.0])


def pack_fp4(w):
    k, n = w.shape
    w = f64(np.asarray(w, np.float32).astype(ml_dtypes.bfloat16)).reshape(k // 32, 32, n)
    amax = np.abs(w).max(1)
    mant, ex = np.frexp(amax / 6.0)
    byte = np.clip(np.where(amax > 0, np.where(mant > 0.5, ex, ex - 1) + 127, 1), 1, 254)
    scaled = (w * np.exp2(127.0 - byte)[:, None, :]).reshape(k, n).astype(np.float32)
    c = np.ascontiguousarray(scaled.reshape(k // 512, 128, 4, n).transpose(0, 1, 3, 2)).astype(ml_dtypes.float4_e2m1fn).view(np.uint8) & 0xF
    words = (c[..., 0::2] | (c[..., 1::2] << 4)).reshape(k // 512, 128, 2 * n)
    return np.ascontiguousarray(words), np.ascontiguousarray(byte.astype(np.uint8).reshape(k // 512, 16, n))


def unpack_fp4(words, scales):
    g, _, n = scales.shape
    words = np.ascontiguousarray(words).reshape(g, 128, n, 2)
    nib = np.empty((g, 128, n, 4), np.uint8)
    nib[..., 0::2] = words & 0xF
    nib[..., 1::2] = words >> 4
    vals = E2M1[nib] * np.repeat(np.exp2(scales.astype(np.float64) - 127.0), 8, axis=1)[..., None]
    return vals.transpose(0, 1, 3, 2).reshape(g * 512, n)


K, T, S, D, V, H, N = 1024, 2048, 1024, 2, 512, 512, 256
P = 2 ** 7


def setup_inputs():
    n = np.random.standard_normal
    s = mx_kscale(K)[:, None]
    u = mx_kscale(H)
    packed_xT = pack_fp4(n((K, T)) * s)
    return {
        "x_words": packed_xT[0],
        "x_scales": packed_xT[1],
        "w1": (n((K, H)) / np.sqrt(K) / s * u).astype(np.float32),
        "w2": (n((H, N)) / np.sqrt(H) / u[:, None]).astype(np.float32),
        "gate": (np.tile(np.random.uniform(0.2, 1.0, (D, 1, V)) / np.sqrt(D), (1, P, 1))).astype(np.float32),
        "offs": striped(np.random.permutation(T)[:S]),
        "cen": striped(np.random.permutation(S)[:V]),
        "pos1": striped(np.random.permutation(S)[:V]),
        "pos2": striped(np.random.permutation(S)[:V]),
    }


def reference(x_words, x_scales, w1, w2, gate, offs, cen, pos1, pos2):
    xq = unpack_fp4(x_words, x_scales)[:, unstriped(offs)]
    h = mxq(f64(w1), 0, "e4m3").T @ xq
    z = h[:, unstriped(cen)] - (h[:, unstriped(pos1)] * f64(gate)[0, :1] + h[:, unstriped(pos2)] * f64(gate)[1, :1])
    return mxq(f64(w2), 0, "e4m3").T @ mxq(z, 0, "e4m3")

@@ -1,0 +1,248 @@
+from contextlib import ExitStack
+
+import concourse.mybir as mybir
+from concourse.masks import make_identity
+
+K, T, S, V, H, N = 1024, 2048, 1024, 512, 512, 256
+FLOPS = 2 * K * H * S + 2 * H * N * V
+
+F32 = mybir.dt.float32
+BF16 = mybir.dt.bfloat16
+I32 = mybir.dt.int32
+U32 = mybir.dt.uint32
+U16 = mybir.dt.uint16
+U8 = mybir.dt.uint8
+FP8X4 = mybir.dt.float8_e4m3fn_x4
+FP4X4 = mybir.dt.float4_e2m1fn_x4
+COPY = mybir.ActivationFunctionType.Copy
+
+P = 128
+PACK = 4
+BANK = 512
+PASSES = K // (P * PACK)
+CHUNKS = (256, 128, 128)
+STAGE_BANKS = (6, 7, 6, 7, 0, 1, 2, 3, 6, 7, 0, 1, 3, 6, 7, 0)
+Z_BANKS = (4, 5, 2, 1)
+OUT_BANKS = (4, 5, 4)
+ADD = mybir.AluOpType.add
+
+
+def tile_picked_lapl_none_p_kernel(
+    tc, x_words, x_scales, w1, w2, gate, offs, cen, pos1, pos2, out
+):
+    nc = tc.nc
+    with ExitStack() as ctx:
+        keep = ctx.enter_context(tc.tile_pool(name="keep", bufs=1))
+        psum = ctx.enter_context(tc.psum_pool(name="psum", bufs=1))
+
+        def bank(b, name):
+            return psum.tile([P, BANK], F32, name=name, tag="bank%d" % b)
+
+        def sb(shape, dtype, name):
+            return keep.tile(shape, dtype, name=name, align_bytes=64)
+
+        scale_table = sb([P, T], U8, "scale_table")
+        nc.gpsimd.memset(scale_table[:].bitcast(I32), 0)
+        scales_1 = sb([P, S], U8, "scales_1")
+        nc.vector.memset(scales_1[:].bitcast(I32), 0)
+        offs_sb = keep.tile([P, S // 16], U16, name="offs_sb")
+        nc.sync.dma_start(offs_sb[:], offs)
+
+        word_table = [sb([P, T], U16, "word_table%d" % g) for g in range(PASSES)]
+        w1_raw = {}
+
+        def load_w1(g, c):
+            w1_raw[g, c] = sb([P, PACK, 256], F32, "w1_raw%d%d" % (g, c))
+            rows = w1[512 * g : 512 * (g + 1), 256 * c : 256 * (c + 1)]
+            nc.sync.dma_start(out=w1_raw[g, c][:], in_=rows.rearrange("(p j) c -> p j c", j=PACK))
+
+        nc.sync.dma_start(out=word_table[0][:].bitcast(I32), in_=x_words[0].bitcast(I32))
+        for q in range(4):
+            nc.sync.dma_start(
+                out=scale_table[32 * q : 32 * q + 8, :].bitcast(I32),
+                in_=x_scales[:, 4 * q : 4 * q + 4, :].bitcast(I32),
+            )
+        load_w1(0, 0)
+        load_w1(0, 1)
+        gate_rows = sb([P, P], F32, "gate_rows")
+        nc.gpsimd.memset(gate_rows[:], 0.0)
+        nc.sync.dma_start(out=gate_rows[0:8, :], in_=gate[:, 0, :].rearrange("d (b c) -> d b c", c=P))
+        load_w1(1, 0)
+        nc.sync.dma_start(out=word_table[1][:].bitcast(I32), in_=x_words[1].bitcast(I32))
+        load_w1(1, 1)
+
+        lists = []
+        for name, src in (("pos1_sb", pos1), ("pos2_sb", pos2), ("cen_sb", cen)):
+            t_ = keep.tile([P, V // 16], U16, name=name)
+            nc.sync.dma_start(t_[:], src)
+            lists.append(t_)
+
+        ident = sb([P, P], F32, "ident")
+        make_identity(nc, ident[:])
+        w2_raw = sb([P, PACK, N], F32, "w2_raw")
+        nc.sync.dma_start(out=w2_raw[:], in_=w2.rearrange("(p j) n -> p j n", j=PACK))
+
+        scales_0 = sb([P, S], U8, "scales_0")
+        nc.vector.tensor_copy(scales_0[:], scale_table[:].indirect(offs_sb[:]))
+        for q in range(4):
+            nc.sync.dma_start(
+                out=scales_1[32 * q : 32 * q + 4, :].bitcast(I32),
+                in_=scales_0[32 * q + 4 : 32 * q + 8, :].bitcast(I32),
+            )
+        x_scale = [scales_0, scales_1]
+
+        x_code = {}
+        w1_code = [sb([P, H], U32, "w1_code%d" % g) for g in range(PASSES)]
+        w1_scale = [sb([P, H], U8, "w1_scale%d" % g) for g in range(PASSES)]
+        for g in range(PASSES):
+            x_code[g] = keep.tile([P, S], U16, name="x_code%d" % g, tag="shared%d" % g, align_bytes=64)
+            for half in range(2):
+                nc.vector.tensor_copy(
+                    x_code[g][:, BANK * half : BANK * (half + 1)],
+                    word_table[g][:].indirect(offs_sb[:, 32 * half : 32 * (half + 1)]),
+                )
+            grouped = keep.tile([P, H * PACK], BF16, name="w1_grouped%d" % g, tag="shared%d" % (g + 1), align_bytes=64)
+            view = grouped[:].rearrange("p (t m j) -> p m j t", t=PACK, j=PACK)
+            for c in range(2):
+                nc.scalar.copy(
+                    out=view[:, 64 * c : 64 * (c + 1)],
+                    in_=w1_raw[g, c][:].rearrange("p j (m t) -> p m j t", t=PACK),
+                )
+            spans = ((0, 512),) if g == 0 else ((0, 128), (128, 256), (256, 512))
+            for a, b in spans:
+                nc.vector.quantize_mx(
+                    out=w1_code[g][:, a:b].bitcast(FP8X4),
+                    scales=w1_scale[g][:, a:b],
+                    in_=grouped[:, PACK * a : PACK * b],
+                )
+
+        h = [sb([P, S], F32, "h%d" % t) for t in range(PACK)]
+        w2_grouped = sb([P, N * PACK], BF16, "w2_grouped")
+        nc.scalar.copy(
+            out=w2_grouped[:].rearrange("p (c i j) -> p c j i", i=4, j=PACK),
+            in_=w2_raw[:].rearrange("p j (c i) -> p c j i", i=4),
+        )
+        for pair in range(2):
+            h_bank = {(t, half): bank(2 * t + half, "h_bank%d%d%d" % (pair, t, half)) for t in range(2) for half in range(2)}
+            for g in range(PASSES):
+                for tt in range(2):
+                    t = 2 * pair + tt
+                    for half in range(2):
+                        nc.tensor.matmul_mx(
+                            out=h_bank[tt, half][:],
+                            lhsT=w1_code[g][:, P * t : P * (t + 1)].bitcast(FP8X4),
+                            lhsT_scale=w1_scale[g][:, P * t : P * (t + 1)],
+                            rhs=x_code[g][:, BANK * half : BANK * (half + 1)].bitcast(FP4X4),
+                            rhs_scale=x_scale[g][:, BANK * half : BANK * (half + 1)],
+                            start=(g == 0),
+                            stop=(g == PASSES - 1),
+                        )
+            for tt in range(2):
+                t = 2 * pair + tt
+                for half in range(2):
+                    dst = h[t][:, BANK * half : BANK * (half + 1)]
+                    if (t, half) == (0, 1):
+                        nc.vector.tensor_copy(dst, h_bank[tt, half][:])
+                    else:
+                        nc.scalar.copy(dst, h_bank[tt, half][:])
+        w2_code = sb([P, N], U32, "w2_code")
+        w2_scale = sb([P, N], U8, "w2_scale")
+        nc.vector.quantize_mx(out=w2_code[:].bitcast(FP8X4), scales=w2_scale[:], in_=w2_grouped[:])
+
+        gate_bank = bank(4, "gate_bank")
+        nc.tensor.transpose(gate_bank[:, 0:P], gate_rows[:], ident[:])
+        neg_gate = sb([P, 8], F32, "neg_gate")
+        nc.scalar.activation(neg_gate[:], gate_bank[:, 0:8], COPY, scale=-1.0)
+
+        turn = 0
+        v0 = 0
+        for ci, width in enumerate(CHUNKS):
+            blocks = width // P
+            b0 = v0 // P
+            z_bank = [bank(Z_BANKS[b0 + b], "z_bank%d" % (b0 + b)) for b in range(blocks)]
+            last = ci == len(CHUNKS) - 1
+            terms = 2 if last else 3
+            for t in range(PACK):
+                turned = []
+                slots = []
+                for li in range(terms):
+                    picked = keep.tile([P, width], F32, name="picked%d%d%d" % (ci, t, li), tag="picked%d" % li, bufs=2, align_bytes=64)
+                    nc.vector.tensor_copy(
+                        picked[:], h[t][:].indirect(lists[li][:, v0 // 16 : (v0 + width) // 16])
+                    )
+                    if li == 0 or (li == 2 and blocks == 2):
+                        stage = bank(STAGE_BANKS[turn], "stage%d" % turn)
+                        turn = turn + 1
+                        col = 0
+                    for b in range(blocks):
+                        nc.tensor.transpose(
+                            stage[:, col + P * b : col + P * (b + 1)], picked[:, P * b : P * (b + 1)], ident[:]
+                        )
+                    slots.append((stage, col))
+                    col = col + width
+                for li in range(terms):
+                    stage_li, col_li = slots[li]
+                    term = sb([P, width], F32, "term%d%d%d" % (ci, t, li))
+                    if li == 2:
+                        nc.scalar.copy(term[:], stage_li[:, col_li : col_li + width])
+                    else:
+                        for b in range(blocks):
+                            gcol = 4 * li + b0 + b
+                            nc.scalar.activation(
+                                term[:, P * b : P * (b + 1)],
+                                stage_li[:, col_li + P * b : col_li + P * (b + 1)],
+                                COPY,
+                                scale=neg_gate[:, gcol : gcol + 1],
+                            )
+                    turned.append(term)
+                for b in range(blocks):
+                    for li in range(terms):
+                        nc.tensor.matmul(
+                            z_bank[b][:, P * t : P * (t + 1)],
+                            lhsT=turned[li][:, P * b : P * (b + 1)],
+                            rhs=ident[:],
+                            is_transpose=True,
+                            start=(li == 0),
+                            stop=(li == terms - 1),
+                        )
+            z_grouped = sb([P, width * PACK], BF16, "z_grouped%d" % ci)
+            if last:
+                centre = keep.tile([P, PACK * width], F32, name="centre", tag="picked0", bufs=2, align_bytes=64)
+                for t in range(PACK):
+                    nc.vector.tensor_copy(
+                        centre[:, width * t : width * (t + 1)],
+                        h[t][:].indirect(lists[2][:, v0 // 16 : (v0 + width) // 16]),
+                    )
+                nc.vector.tensor_tensor(
+                    z_grouped[:].rearrange("p (c i t) -> p c t i", i=4, t=PACK),
+                    z_bank[0][:].rearrange("p (t c i) -> p c t i", i=4, t=PACK),
+                    centre[:].rearrange("p (t c i) -> p c t i", i=4, t=PACK),
+                    ADD,
+                )
+            else:
+                for b in range(blocks):
+                    nc.scalar.copy(
+                        out=z_grouped[:, BANK * b : BANK * (b + 1)].rearrange("p (v t) -> p v t", t=PACK),
+                        in_=z_bank[b][:].rearrange("p (t v) -> p v t", t=PACK),
+                    )
+            z_code = sb([P, width], U32, "z_code%d" % ci)
+            z_scale = sb([P, width], U8, "z_scale%d" % ci)
+            nc.vector.quantize_mx(out=z_code[:].bitcast(FP8X4), scales=z_scale[:], in_=z_grouped[:])
+            out_bank = bank(OUT_BANKS[ci], "out_bank%d" % ci)
+            for a in range(N // P):
+                nc.tensor.matmul_mx(
+                    out=out_bank[:, width * a : width * (a + 1)],
+                    lhsT=w2_code[:, P * a : P * (a + 1)].bitcast(FP8X4),
+                    lhsT_scale=w2_scale[:, P * a : P * (a + 1)],
+                    rhs=z_code[:].bitcast(FP8X4),
+                    rhs_scale=z_scale[:],
+                    start=True,
+                    stop=True,
+                )
+            result = sb([P, 2 * width], F32, "result%d" % ci)
+            nc.scalar.copy(result[:], out_bank[:, 0 : 2 * width])
+            nc.sync.dma_start(
+                out=out.rearrange("(a p) v -> p a v", p=P)[:, :, v0 : v0 + width],
+                in_=result[:].rearrange("p (a v) -> p a v", a=2),
+            )
+            v0 = v0 + width

@@ -21,9 +21,10 @@ PACK = 4
 BANK = 512
 PASSES = K // (P * PACK)
 CHUNKS = (256, 128, 128)
-STAGE_BANKS = (6, 7, 6, 7, 0, 1, 2, 3, 6, 7, 0, 1, 3, 6, 7, 0)
-Z_BANKS = (4, 5, 2, 1)
-OUT_BANKS = (4, 5, 4)
+H_BANKS = (0, 2, 4, 0)
+STAGE_BANKS = (6, 3, 4, 5)
+Z_BANKS = (7, 2, 0, 1)
+OUT_BANKS = (7, 2, 7)
 ADD = mybir.AluOpType.add
 
 
@@ -80,7 +81,8 @@ def tile_picked_lapl_none_p_kernel(
         ident = sb([P, P], F32, "ident")
         make_identity(nc, ident[:])
         w2_raw = sb([P, PACK, N], F32, "w2_raw")
-        nc.sync.dma_start(out=w2_raw[:], in_=w2.rearrange("(p j) n -> p j n", j=PACK))
+        for t in range(PACK):
+            nc.sync.dma_start(out=w2_raw[:, t, :], in_=w2.rearrange("(q t r) n -> t q r n", t=PACK, r=8)[t])
 
         scales_0 = sb([P, S], U8, "scales_0")
         nc.vector.tensor_copy(scales_0[:], scale_table[:].indirect(offs_sb[:]))
@@ -102,11 +104,11 @@ def tile_picked_lapl_none_p_kernel(
                     word_table[g][:].indirect(offs_sb[:, 32 * half : 32 * (half + 1)]),
                 )
             grouped = keep.tile([P, H * PACK], BF16, name="w1_grouped%d" % g, tag="shared%d" % (g + 1), align_bytes=64)
-            view = grouped[:].rearrange("p (t m j) -> p m j t", t=PACK, j=PACK)
+            view = grouped[:].rearrange("p (t q r j) -> p t q r j", t=PACK, r=8, j=PACK)
             for c in range(2):
                 nc.scalar.copy(
-                    out=view[:, 64 * c : 64 * (c + 1)],
-                    in_=w1_raw[g, c][:].rearrange("p j (m t) -> p m j t", t=PACK),
+                    out=view[:, :, 8 * c : 8 * (c + 1)],
+                    in_=w1_raw[g, c][:].rearrange("p j (q t r) -> p t q r j", t=PACK, r=8),
                 )
             spans = ((0, 512),) if g == 0 else ((0, 128), (128, 256), (256, 512))
             for a, b in spans:
@@ -122,14 +124,15 @@ def tile_picked_lapl_none_p_kernel(
             out=w2_grouped[:].rearrange("p (c i j) -> p c j i", i=4, j=PACK),
             in_=w2_raw[:].rearrange("p j (c i) -> p c j i", i=4),
         )
-        for pair in range(2):
-            h_bank = {(t, half): bank(2 * t + half, "h_bank%d%d%d" % (pair, t, half)) for t in range(2) for half in range(2)}
+        for group in ((0, 1, 2), (3,)):
+            h_bank = {
+                (t, half): bank(H_BANKS[t] + half, "h_bank%d%d" % (t, half)) for t in group for half in range(2)
+            }
             for g in range(PASSES):
-                for tt in range(2):
-                    t = 2 * pair + tt
+                for t in group:
                     for half in range(2):
                         nc.tensor.matmul_mx(
-                            out=h_bank[tt, half][:],
+                            out=h_bank[t, half][:],
                             lhsT=w1_code[g][:, P * t : P * (t + 1)].bitcast(FP8X4),
                             lhsT_scale=w1_scale[g][:, P * t : P * (t + 1)],
                             rhs=x_code[g][:, BANK * half : BANK * (half + 1)].bitcast(FP4X4),
@@ -137,93 +140,86 @@ def tile_picked_lapl_none_p_kernel(
                             start=(g == 0),
                             stop=(g == PASSES - 1),
                         )
-            for tt in range(2):
-                t = 2 * pair + tt
+            for t in group:
                 for half in range(2):
                     dst = h[t][:, BANK * half : BANK * (half + 1)]
                     if (t, half) == (0, 1):
-                        nc.vector.tensor_copy(dst, h_bank[tt, half][:])
+                        nc.vector.tensor_copy(dst, h_bank[t, half][:])
                     else:
-                        nc.scalar.copy(dst, h_bank[tt, half][:])
+                        nc.scalar.copy(dst, h_bank[t, half][:])
         w2_code = sb([P, N], U32, "w2_code")
         w2_scale = sb([P, N], U8, "w2_scale")
         nc.vector.quantize_mx(out=w2_code[:].bitcast(FP8X4), scales=w2_scale[:], in_=w2_grouped[:])
 
-        gate_bank = bank(4, "gate_bank")
+        gate_bank = bank(6, "gate_bank")
         nc.tensor.transpose(gate_bank[:, 0:P], gate_rows[:], ident[:])
         neg_gate = sb([P, 8], F32, "neg_gate")
         nc.scalar.activation(neg_gate[:], gate_bank[:, 0:8], COPY, scale=-1.0)
 
-        turn = 0
         v0 = 0
         for ci, width in enumerate(CHUNKS):
             blocks = width // P
             b0 = v0 // P
             z_bank = [bank(Z_BANKS[b0 + b], "z_bank%d" % (b0 + b)) for b in range(blocks)]
             last = ci == len(CHUNKS) - 1
-            terms = 2 if last else 3
+            columns = slice(v0 // 16, (v0 + width) // 16)
             for t in range(PACK):
-                turned = []
-                slots = []
-                for li in range(terms):
-                    picked = keep.tile([P, width], F32, name="picked%d%d%d" % (ci, t, li), tag="picked%d" % li, bufs=2, align_bytes=64)
-                    nc.vector.tensor_copy(
-                        picked[:], h[t][:].indirect(lists[li][:, v0 // 16 : (v0 + width) // 16])
+                stage = bank(STAGE_BANKS[t], "stage%d%d" % (ci, t))
+                for li in range(2):
+                    picked = keep.tile(
+                        [P, width], F32, name="picked%d%d%d" % (ci, t, li), tag="picked%d" % li, bufs=2, align_bytes=64
                     )
-                    if li == 0 or (li == 2 and blocks == 2):
-                        stage = bank(STAGE_BANKS[turn], "stage%d" % turn)
-                        turn = turn + 1
-                        col = 0
+                    nc.vector.tensor_copy(picked[:], h[t][:].indirect(lists[li][:, columns]))
                     for b in range(blocks):
-                        nc.tensor.transpose(
-                            stage[:, col + P * b : col + P * (b + 1)], picked[:, P * b : P * (b + 1)], ident[:]
+                        col = width * li + P * b
+                        nc.tensor.transpose(stage[:, col : col + P], picked[:, P * b : P * (b + 1)], ident[:])
+                term = sb([P, 2 * width], F32, "term%d%d" % (ci, t))
+                for li in range(2):
+                    for b in range(blocks):
+                        col = width * li + P * b
+                        gcol = 4 * li + b0 + b
+                        nc.scalar.activation(
+                            term[:, col : col + P], stage[:, col : col + P], COPY, scale=neg_gate[:, gcol : gcol + 1]
                         )
-                    slots.append((stage, col))
-                    col = col + width
-                for li in range(terms):
-                    stage_li, col_li = slots[li]
-                    term = sb([P, width], F32, "term%d%d%d" % (ci, t, li))
-                    if li == 2:
-                        nc.scalar.copy(term[:], stage_li[:, col_li : col_li + width])
-                    else:
-                        for b in range(blocks):
-                            gcol = 4 * li + b0 + b
-                            nc.scalar.activation(
-                                term[:, P * b : P * (b + 1)],
-                                stage_li[:, col_li + P * b : col_li + P * (b + 1)],
-                                COPY,
-                                scale=neg_gate[:, gcol : gcol + 1],
-                            )
-                    turned.append(term)
                 for b in range(blocks):
-                    for li in range(terms):
+                    for li in range(2):
+                        col = width * li + P * b
                         nc.tensor.matmul(
                             z_bank[b][:, P * t : P * (t + 1)],
-                            lhsT=turned[li][:, P * b : P * (b + 1)],
+                            lhsT=term[:, col : col + P],
                             rhs=ident[:],
                             is_transpose=True,
                             start=(li == 0),
-                            stop=(li == terms - 1),
+                            stop=(li == 1),
                         )
-            z_grouped = sb([P, width * PACK], BF16, "z_grouped%d" % ci)
             if last:
-                centre = keep.tile([P, PACK * width], F32, name="centre", tag="picked0", bufs=2, align_bytes=64)
-                for t in range(PACK):
-                    nc.vector.tensor_copy(
-                        centre[:, width * t : width * (t + 1)],
-                        h[t][:].indirect(lists[2][:, v0 // 16 : (v0 + width) // 16]),
-                    )
-                nc.vector.tensor_tensor(
-                    z_grouped[:].rearrange("p (c i t) -> p c t i", i=4, t=PACK),
-                    z_bank[0][:].rearrange("p (t c i) -> p c t i", i=4, t=PACK),
-                    centre[:].rearrange("p (t c i) -> p c t i", i=4, t=PACK),
-                    ADD,
-                )
+                centre = keep.tile([P, PACK * width], F32, name="centre%d" % ci, tag="picked0", bufs=2, align_bytes=64)
             else:
-                for b in range(blocks):
+                centre = keep.tile([P, PACK * width], F32, name="centre%d" % ci, tag="centre", align_bytes=64)
+            for t in range(PACK):
+                nc.vector.tensor_copy(centre[:, width * t : width * (t + 1)], h[t][:].indirect(lists[2][:, columns]))
+            z_grouped = sb([P, width * PACK], BF16, "z_grouped%d" % ci)
+            for b in range(blocks):
+                own = centre[:].rearrange("p (t v) -> p t v", t=PACK)[:, :, P * b : P * (b + 1)]
+                grouped_b = z_grouped[:, BANK * b : BANK * (b + 1)]
+                if last:
+                    nc.vector.tensor_tensor(
+                        grouped_b.rearrange("p (c i t) -> p c t i", i=4, t=PACK),
+                        z_bank[b][:].rearrange("p (t c i) -> p c t i", i=4, t=PACK),
+                        own.rearrange("p t (c i) -> p c t i", i=4),
+                        ADD,
+                    )
+                else:
+                    z_sum = sb([P, BANK], F32, "z_sum%d" % (b0 + b))
+                    nc.vector.tensor_tensor(
+                        z_sum[:].rearrange("p (t v) -> p t v", t=PACK),
+                        z_bank[b][:].rearrange("p (t v) -> p t v", t=PACK),
+                        own,
+                        ADD,
+                    )
                     nc.scalar.copy(
-                        out=z_grouped[:, BANK * b : BANK * (b + 1)].rearrange("p (v t) -> p v t", t=PACK),
-                        in_=z_bank[b][:].rearrange("p (t v) -> p v t", t=PACK),
+                        out=grouped_b.rearrange("p (v t) -> p v t", t=PACK),
+                        in_=z_sum[:].rearrange("p (t v) -> p v t", t=PACK),
                     )
             z_code = sb([P, width], U32, "z_code%d" % ci)
             z_scale = sb([P, width], U8, "z_scale%d" % ci)

@@ -20,11 +20,11 @@ P = 128
 PACK = 4
 BANK = 512
 PASSES = K // (P * PACK)
-CHUNKS = (256, 128, 128)
+CHUNK = 256
 H_BANKS = (0, 2, 4, 0)
 STAGE_BANKS = (6, 3, 4, 5)
 Z_BANKS = (7, 2, 0, 1)
-OUT_BANKS = (7, 2, 7)
+OUT_BANKS = (7, 2, 6)
 ADD = mybir.AluOpType.add
 
 
@@ -42,47 +42,46 @@ def tile_picked_lapl_none_p_kernel(
         def sb(shape, dtype, name):
             return keep.tile(shape, dtype, name=name, align_bytes=64)
 
-        scale_table = sb([P, T], U8, "scale_table")
+        scale_table = keep.tile([P, T], U8, name="scale_table", tag="early", align_bytes=64)
         nc.gpsimd.memset(scale_table[:].bitcast(I32), 0)
         scales_1 = sb([P, S], U8, "scales_1")
         nc.vector.memset(scales_1[:].bitcast(I32), 0)
-        offs_sb = keep.tile([P, S // 16], U16, name="offs_sb")
-        nc.sync.dma_start(offs_sb[:], offs)
 
-        word_table = [sb([P, T], U16, "word_table%d" % g) for g in range(PASSES)]
-        w1_raw = {}
+        def load_list(name, src):
+            tile = keep.tile([P, src.shape[1]], U16, name=name)
+            nc.sync.dma_start(tile[:], src)
+            return tile
 
-        def load_w1(g, c):
-            w1_raw[g, c] = sb([P, PACK, 256], F32, "w1_raw%d%d" % (g, c))
-            rows = w1[512 * g : 512 * (g + 1), 256 * c : 256 * (c + 1)]
-            nc.sync.dma_start(out=w1_raw[g, c][:], in_=rows.rearrange("(p j) c -> p j c", j=PACK))
+        word_table = [
+            keep.tile([P, T], U16, name="word_table%d" % g, tag="words%d" % g, align_bytes=64) for g in range(PASSES)
+        ]
+        w1_raw = [sb([P, PACK, H], F32, "w1_raw%d" % g) for g in range(PASSES)]
 
-        nc.sync.dma_start(out=word_table[0][:].bitcast(I32), in_=x_words[0].bitcast(I32))
+        def load_words(g):
+            nc.sync.dma_start(out=word_table[g][:].bitcast(I32), in_=x_words[g].bitcast(I32))
+
+        def load_w1(g):
+            rows = w1[512 * g : 512 * (g + 1), :]
+            nc.sync.dma_start(out=w1_raw[g][:], in_=rows.rearrange("(p j) c -> p j c", j=PACK))
+
+        offs_sb = load_list("offs_sb", offs)
+        load_words(0)
         for q in range(4):
             nc.sync.dma_start(
                 out=scale_table[32 * q : 32 * q + 8, :].bitcast(I32),
                 in_=x_scales[:, 4 * q : 4 * q + 4, :].bitcast(I32),
             )
-        load_w1(0, 0)
-        load_w1(0, 1)
-        gate_rows = sb([P, P], F32, "gate_rows")
-        nc.gpsimd.memset(gate_rows[:], 0.0)
-        nc.sync.dma_start(out=gate_rows[0:8, :], in_=gate[:, 0, :].rearrange("d (b c) -> d b c", c=P))
-        load_w1(1, 0)
-        nc.sync.dma_start(out=word_table[1][:].bitcast(I32), in_=x_words[1].bitcast(I32))
-        load_w1(1, 1)
-
-        lists = []
-        for name, src in (("pos1_sb", pos1), ("pos2_sb", pos2), ("cen_sb", cen)):
-            t_ = keep.tile([P, V // 16], U16, name=name)
-            nc.sync.dma_start(t_[:], src)
-            lists.append(t_)
+        lists = [load_list("pos1_sb", pos1), load_list("pos2_sb", pos2)]
+        load_w1(0)
+        load_words(1)
+        load_w1(1)
+        cen_sb = load_list("cen_sb", cen)
 
         ident = sb([P, P], F32, "ident")
         make_identity(nc, ident[:])
-        w2_raw = sb([P, PACK, N], F32, "w2_raw")
-        for t in range(PACK):
-            nc.sync.dma_start(out=w2_raw[:, t, :], in_=w2.rearrange("(q t r) n -> t q r n", t=PACK, r=8)[t])
+        gate_rows = sb([P, P], F32, "gate_rows")
+        nc.gpsimd.memset(gate_rows[:], 0.0)
+        nc.sync.dma_start(out=gate_rows[0:8, :], in_=gate[:, 0, :].rearrange("d (b c) -> d b c", c=P))
 
         scales_0 = sb([P, S], U8, "scales_0")
         nc.vector.tensor_copy(scales_0[:], scale_table[:].indirect(offs_sb[:]))
@@ -96,27 +95,32 @@ def tile_picked_lapl_none_p_kernel(
         x_code = {}
         w1_code = [sb([P, H], U32, "w1_code%d" % g) for g in range(PASSES)]
         w1_scale = [sb([P, H], U8, "w1_scale%d" % g) for g in range(PASSES)]
+        code_tags = {(0, 0): "codes", (0, 1): "early", (1, 0): "grouped00", (1, 1): "grouped01"}
         for g in range(PASSES):
-            x_code[g] = keep.tile([P, S], U16, name="x_code%d" % g, tag="shared%d" % g, align_bytes=64)
             for half in range(2):
+                x_code[g, half] = keep.tile(
+                    [P, BANK], U16, name="x_code%d%d" % (g, half), tag=code_tags[g, half], align_bytes=64
+                )
                 nc.vector.tensor_copy(
-                    x_code[g][:, BANK * half : BANK * (half + 1)],
-                    word_table[g][:].indirect(offs_sb[:, 32 * half : 32 * (half + 1)]),
+                    x_code[g, half][:], word_table[g][:].indirect(offs_sb[:, 32 * half : 32 * (half + 1)])
                 )
-            grouped = keep.tile([P, H * PACK], BF16, name="w1_grouped%d" % g, tag="shared%d" % (g + 1), align_bytes=64)
-            view = grouped[:].rearrange("p (t q r j) -> p t q r j", t=PACK, r=8, j=PACK)
-            for c in range(2):
-                nc.scalar.copy(
-                    out=view[:, :, 8 * c : 8 * (c + 1)],
-                    in_=w1_raw[g, c][:].rearrange("p j (q t r) -> p t q r j", t=PACK, r=8),
-                )
-            spans = ((0, 512),) if g == 0 else ((0, 128), (128, 256), (256, 512))
-            for a, b in spans:
-                nc.vector.quantize_mx(
-                    out=w1_code[g][:, a:b].bitcast(FP8X4),
-                    scales=w1_scale[g][:, a:b],
-                    in_=grouped[:, PACK * a : PACK * b],
-                )
+            dealt = w1_raw[g][:].rearrange("p j (q t r) -> p t q r j", t=PACK, r=8)
+            for pair in range(2):
+                name = "grouped%d%d" % (g, pair)
+                grouped = keep.tile([P, 2 * BANK], BF16, name=name, tag=name, align_bytes=64)
+                view = grouped[:].rearrange("p (t q r j) -> p t q r j", t=2, r=8, j=PACK)
+                for tt in range(2):
+                    nc.scalar.copy(out=view[:, tt], in_=dealt[:, 2 * pair + tt])
+                for a, b in ((0, 256),) if g == 0 else ((0, 128), (128, 256)):
+                    nc.vector.quantize_mx(
+                        out=w1_code[g][:, 256 * pair + a : 256 * pair + b].bitcast(FP8X4),
+                        scales=w1_scale[g][:, 256 * pair + a : 256 * pair + b],
+                        in_=grouped[:, PACK * a : PACK * b],
+                    )
+        w2_raw = keep.tile([P, PACK, N], F32, name="w2_raw", tag="words0", align_bytes=64)
+        for t in range(PACK):
+            nc.sync.dma_start(out=w2_raw[:, t, :], in_=w2.rearrange("(q t r) n -> t q r n", t=PACK, r=8)[t])
+
 
         h = [sb([P, S], F32, "h%d" % t) for t in range(PACK)]
         w2_grouped = sb([P, N * PACK], BF16, "w2_grouped")
@@ -135,7 +139,7 @@ def tile_picked_lapl_none_p_kernel(
                             out=h_bank[t, half][:],
                             lhsT=w1_code[g][:, P * t : P * (t + 1)].bitcast(FP8X4),
                             lhsT_scale=w1_scale[g][:, P * t : P * (t + 1)],
-                            rhs=x_code[g][:, BANK * half : BANK * (half + 1)].bitcast(FP4X4),
+                            rhs=x_code[g, half][:].bitcast(FP4X4),
                             rhs_scale=x_scale[g][:, BANK * half : BANK * (half + 1)],
                             start=(g == 0),
                             stop=(g == PASSES - 1),
@@ -156,75 +160,54 @@ def tile_picked_lapl_none_p_kernel(
         neg_gate = sb([P, 8], F32, "neg_gate")
         nc.scalar.activation(neg_gate[:], gate_bank[:, 0:8], COPY, scale=-1.0)
 
-        v0 = 0
-        for ci, width in enumerate(CHUNKS):
-            blocks = width // P
-            b0 = v0 // P
-            z_bank = [bank(Z_BANKS[b0 + b], "z_bank%d" % (b0 + b)) for b in range(blocks)]
-            last = ci == len(CHUNKS) - 1
-            columns = slice(v0 // 16, (v0 + width) // 16)
+        blocks = CHUNK // P
+        z_bank = {}
+
+        def turn_neighbours(ci):
+            columns = slice(ci * CHUNK // 16, (ci + 1) * CHUNK // 16)
+            for b in range(blocks):
+                z_bank[ci, b] = bank(Z_BANKS[blocks * ci + b], "z_bank%d%d" % (ci, b))
             for t in range(PACK):
                 stage = bank(STAGE_BANKS[t], "stage%d%d" % (ci, t))
                 for li in range(2):
                     picked = keep.tile(
-                        [P, width], F32, name="picked%d%d%d" % (ci, t, li), tag="picked%d" % li, bufs=2, align_bytes=64
+                        [P, CHUNK], F32, name="picked%d%d%d" % (ci, t, li), tag="picked%d" % li, bufs=2, align_bytes=64
                     )
                     nc.vector.tensor_copy(picked[:], h[t][:].indirect(lists[li][:, columns]))
                     for b in range(blocks):
-                        col = width * li + P * b
+                        col = CHUNK * li + P * b
                         nc.tensor.transpose(stage[:, col : col + P], picked[:, P * b : P * (b + 1)], ident[:])
-                term = sb([P, 2 * width], F32, "term%d%d" % (ci, t))
-                for li in range(2):
-                    for b in range(blocks):
-                        col = width * li + P * b
-                        gcol = 4 * li + b0 + b
+                term = sb([P, 2 * CHUNK], F32, "term%d%d" % (ci, t))
+                for b in range(blocks):
+                    for li in range(2):
+                        col = CHUNK * li + P * b
+                        gcol = 4 * li + blocks * ci + b
                         nc.scalar.activation(
                             term[:, col : col + P], stage[:, col : col + P], COPY, scale=neg_gate[:, gcol : gcol + 1]
                         )
                 for b in range(blocks):
                     for li in range(2):
-                        col = width * li + P * b
+                        col = CHUNK * li + P * b
                         nc.tensor.matmul(
-                            z_bank[b][:, P * t : P * (t + 1)],
+                            z_bank[ci, b][:, P * t : P * (t + 1)],
                             lhsT=term[:, col : col + P],
                             rhs=ident[:],
                             is_transpose=True,
                             start=(li == 0),
                             stop=(li == 1),
                         )
-            if last:
-                centre = keep.tile([P, PACK * width], F32, name="centre%d" % ci, tag="picked0", bufs=2, align_bytes=64)
-            else:
-                centre = keep.tile([P, PACK * width], F32, name="centre%d" % ci, tag="centre", align_bytes=64)
+
+        def gather_centres(ci, centre):
+            columns = slice(ci * CHUNK // 16, (ci + 1) * CHUNK // 16)
             for t in range(PACK):
-                nc.vector.tensor_copy(centre[:, width * t : width * (t + 1)], h[t][:].indirect(lists[2][:, columns]))
-            z_grouped = sb([P, width * PACK], BF16, "z_grouped%d" % ci)
-            for b in range(blocks):
-                own = centre[:].rearrange("p (t v) -> p t v", t=PACK)[:, :, P * b : P * (b + 1)]
-                grouped_b = z_grouped[:, BANK * b : BANK * (b + 1)]
-                if last:
-                    nc.vector.tensor_tensor(
-                        grouped_b.rearrange("p (c i t) -> p c t i", i=4, t=PACK),
-                        z_bank[b][:].rearrange("p (t c i) -> p c t i", i=4, t=PACK),
-                        own.rearrange("p t (c i) -> p c t i", i=4),
-                        ADD,
-                    )
-                else:
-                    z_sum = sb([P, BANK], F32, "z_sum%d" % (b0 + b))
-                    nc.vector.tensor_tensor(
-                        z_sum[:].rearrange("p (t v) -> p t v", t=PACK),
-                        z_bank[b][:].rearrange("p (t v) -> p t v", t=PACK),
-                        own,
-                        ADD,
-                    )
-                    nc.scalar.copy(
-                        out=grouped_b.rearrange("p (v t) -> p v t", t=PACK),
-                        in_=z_sum[:].rearrange("p (t v) -> p v t", t=PACK),
-                    )
-            z_code = sb([P, width], U32, "z_code%d" % ci)
-            z_scale = sb([P, width], U8, "z_scale%d" % ci)
+                nc.vector.tensor_copy(centre[:, CHUNK * t : CHUNK * (t + 1)], h[t][:].indirect(cen_sb[:, columns]))
+            return centre[:].rearrange("p (t v) -> p t v", t=PACK)
+
+        def project(piece, z_grouped, v0, width):
+            z_code = sb([P, width], U32, "z_code%d" % piece)
+            z_scale = sb([P, width], U8, "z_scale%d" % piece)
             nc.vector.quantize_mx(out=z_code[:].bitcast(FP8X4), scales=z_scale[:], in_=z_grouped[:])
-            out_bank = bank(OUT_BANKS[ci], "out_bank%d" % ci)
+            out_bank = bank(OUT_BANKS[piece], "out_bank%d" % piece)
             for a in range(N // P):
                 nc.tensor.matmul_mx(
                     out=out_bank[:, width * a : width * (a + 1)],
@@ -235,10 +218,41 @@ def tile_picked_lapl_none_p_kernel(
                     start=True,
                     stop=True,
                 )
-            result = sb([P, 2 * width], F32, "result%d" % ci)
+            result = sb([P, 2 * width], F32, "result%d" % piece)
             nc.scalar.copy(result[:], out_bank[:, 0 : 2 * width])
             nc.sync.dma_start(
                 out=out.rearrange("(a p) v -> p a v", p=P)[:, :, v0 : v0 + width],
                 in_=result[:].rearrange("p (a v) -> p a v", a=2),
             )
-            v0 = v0 + width
+
+        turn_neighbours(0)
+        centre_0 = gather_centres(0, sb([P, PACK * CHUNK], F32, "centre0"))
+        z_grouped_0 = keep.tile([P, CHUNK * PACK], BF16, name="z_grouped0", tag="late", align_bytes=64)
+        for b in range(blocks):
+            z_sum = sb([P, BANK], F32, "z_sum%d" % b)
+            nc.vector.tensor_tensor(
+                z_sum[:].rearrange("p (t v) -> p t v", t=PACK),
+                z_bank[0, b][:].rearrange("p (t v) -> p t v", t=PACK),
+                centre_0[:, :, P * b : P * (b + 1)],
+                ADD,
+            )
+            nc.scalar.copy(
+                out=z_grouped_0[:, BANK * b : BANK * (b + 1)].rearrange("p (v t) -> p v t", t=PACK),
+                in_=z_sum[:].rearrange("p (t v) -> p v t", t=PACK),
+            )
+        project(0, z_grouped_0, 0, CHUNK)
+
+        turn_neighbours(1)
+        centre_1 = gather_centres(
+            1, keep.tile([P, PACK * CHUNK], F32, name="centre1", tag="late", align_bytes=64)
+        )
+        z_grouped_1 = [sb([P, BANK], BF16, "z_grouped1%d" % b) for b in range(blocks)]
+        for b in range(blocks):
+            nc.vector.tensor_tensor(
+                z_grouped_1[b][:].rearrange("p (c i t) -> p c t i", i=4, t=PACK),
+                z_bank[1, b][:].rearrange("p (t c i) -> p c t i", i=4, t=PACK),
+                centre_1[:, :, P * b : P * (b + 1)].rearrange("p t (c i) -> p c t i", i=4),
+                ADD,
+            )
+        for b in range(blocks):
+            project(1 + b, z_grouped_1[b], CHUNK + P * b, P)

@@ -15,17 +15,24 @@ U8 = mybir.dt.uint8
 FP8X4 = mybir.dt.float8_e4m3fn_x4
 FP4X4 = mybir.dt.float4_e2m1fn_x4
 COPY = mybir.ActivationFunctionType.Copy
+ADD = mybir.AluOpType.add
 
 P = 128
 PACK = 4
 BANK = 512
 PASSES = K // (P * PACK)
+QUADRANTS = 4
+BLOCK_ROWS = 8
+LIST_ROWS = 16
 CHUNK = 256
-H_BANKS = (0, 2, 4, 0)
-STAGE_BANKS = (6, 3, 4, 5)
-Z_BANKS = (7, 2, 0, 1)
-OUT_BANKS = (7, 2, 6)
-ADD = mybir.AluOpType.add
+BLOCKS = CHUNK // P
+GATE_COLUMNS = V // P
+
+H_BANKS = (0, 2, 0, 2)
+GATE_BANK = 4
+STAGE_BANKS = (4, 5, 0, 1)
+SUM_BANKS = (6, 7, 2, 3)
+OUT_BANKS = (6, 7, 4)
 
 
 def tile_picked_lapl_none_p_kernel(
@@ -36,14 +43,15 @@ def tile_picked_lapl_none_p_kernel(
         keep = ctx.enter_context(tc.tile_pool(name="keep", bufs=1))
         psum = ctx.enter_context(tc.psum_pool(name="psum", bufs=1))
 
-        def bank(b, name):
-            return psum.tile([P, BANK], F32, name=name, tag="bank%d" % b)
+        def bank(number, name):
+            return psum.tile([P, BANK], F32, name=name, tag="bank%d" % number)
 
-        def sb(shape, dtype, name):
-            return keep.tile(shape, dtype, name=name, align_bytes=64)
+        def sb(shape, dtype, name, tag="", bufs=1):
+            return keep.tile(shape, dtype, name=name, tag=tag or name, bufs=bufs, align_bytes=64)
 
-        scale_table = keep.tile([P, T], U8, name="scale_table", tag="early", align_bytes=64)
-        nc.gpsimd.memset(scale_table[:].bitcast(I32), 0)
+        scale_table = sb([P, T], U8, "scale_table")
+        nc.gpsimd.memset(scale_table[:, 0 : T // 2].bitcast(I32), 0)
+        nc.vector.memset(scale_table[:, T // 2 : T].bitcast(I32), 0)
         scales_1 = sb([P, S], U8, "scales_1")
         nc.vector.memset(scales_1[:].bitcast(I32), 0)
 
@@ -52,40 +60,40 @@ def tile_picked_lapl_none_p_kernel(
             nc.sync.dma_start(tile[:], src)
             return tile
 
-        word_table = [
-            keep.tile([P, T], U16, name="word_table%d" % g, tag="words%d" % g, align_bytes=64) for g in range(PASSES)
-        ]
+        word_table = [sb([P, T], U16, "word_table%d" % g) for g in range(PASSES)]
         w1_raw = [sb([P, PACK, H], F32, "w1_raw%d" % g) for g in range(PASSES)]
 
         def load_words(g):
             nc.sync.dma_start(out=word_table[g][:].bitcast(I32), in_=x_words[g].bitcast(I32))
 
         def load_w1(g):
-            rows = w1[512 * g : 512 * (g + 1), :]
+            rows = w1[P * PACK * g : P * PACK * (g + 1), :]
             nc.sync.dma_start(out=w1_raw[g][:], in_=rows.rearrange("(p j) c -> p j c", j=PACK))
 
         offs_sb = load_list("offs_sb", offs)
         load_words(0)
-        for q in range(4):
+        for q in range(QUADRANTS):
             nc.sync.dma_start(
-                out=scale_table[32 * q : 32 * q + 8, :].bitcast(I32),
+                out=scale_table[32 * q : 32 * q + 4 * PASSES, :].bitcast(I32),
                 in_=x_scales[:, 4 * q : 4 * q + 4, :].bitcast(I32),
             )
-        lists = [load_list("pos1_sb", pos1), load_list("pos2_sb", pos2)]
         load_w1(0)
         load_words(1)
         load_w1(1)
+        neighbour_lists = [load_list("pos1_sb", pos1), load_list("pos2_sb", pos2)]
         cen_sb = load_list("cen_sb", cen)
 
         ident = sb([P, P], F32, "ident")
         make_identity(nc, ident[:])
         gate_rows = sb([P, P], F32, "gate_rows")
         nc.gpsimd.memset(gate_rows[:], 0.0)
-        nc.sync.dma_start(out=gate_rows[0:8, :], in_=gate[:, 0, :].rearrange("d (b c) -> d b c", c=P))
+        nc.sync.dma_start(
+            out=gate_rows[0 : 2 * GATE_COLUMNS, :], in_=gate[:, 0, :].rearrange("d (b c) -> d b c", c=P)
+        )
 
         scales_0 = sb([P, S], U8, "scales_0")
         nc.vector.tensor_copy(scales_0[:], scale_table[:].indirect(offs_sb[:]))
-        for q in range(4):
+        for q in range(QUADRANTS):
             nc.sync.dma_start(
                 out=scales_1[32 * q : 32 * q + 4, :].bitcast(I32),
                 in_=scales_0[32 * q + 4 : 32 * q + 8, :].bitcast(I32),
@@ -95,45 +103,44 @@ def tile_picked_lapl_none_p_kernel(
         x_code = {}
         w1_code = [sb([P, H], U32, "w1_code%d" % g) for g in range(PASSES)]
         w1_scale = [sb([P, H], U8, "w1_scale%d" % g) for g in range(PASSES)]
-        code_tags = {(0, 0): "codes", (0, 1): "early", (1, 0): "grouped00", (1, 1): "grouped01"}
-        for g in range(PASSES):
-            for half in range(2):
-                x_code[g, half] = keep.tile(
-                    [P, BANK], U16, name="x_code%d%d" % (g, half), tag=code_tags[g, half], align_bytes=64
-                )
-                nc.vector.tensor_copy(
-                    x_code[g, half][:], word_table[g][:].indirect(offs_sb[:, 32 * half : 32 * (half + 1)])
-                )
-            dealt = w1_raw[g][:].rearrange("p j (q t r) -> p t q r j", t=PACK, r=8)
-            for pair in range(2):
-                name = "grouped%d%d" % (g, pair)
-                grouped = keep.tile([P, 2 * BANK], BF16, name=name, tag=name, align_bytes=64)
-                view = grouped[:].rearrange("p (t q r j) -> p t q r j", t=2, r=8, j=PACK)
-                for tt in range(2):
-                    nc.scalar.copy(out=view[:, tt], in_=dealt[:, 2 * pair + tt])
-                for a, b in ((0, 256),) if g == 0 else ((0, 128), (128, 256)):
-                    nc.vector.quantize_mx(
-                        out=w1_code[g][:, 256 * pair + a : 256 * pair + b].bitcast(FP8X4),
-                        scales=w1_scale[g][:, 256 * pair + a : 256 * pair + b],
-                        in_=grouped[:, PACK * a : PACK * b],
-                    )
-        w2_raw = keep.tile([P, PACK, N], F32, name="w2_raw", tag="words0", align_bytes=64)
-        for t in range(PACK):
-            nc.sync.dma_start(out=w2_raw[:, t, :], in_=w2.rearrange("(q t r) n -> t q r n", t=PACK, r=8)[t])
 
+        def gather_words(g, half, behind):
+            x_code[g, half] = sb([P, BANK], U16, "x_code%d%d" % (g, half), tag=behind)
+            columns = slice(half * BANK // LIST_ROWS, (half + 1) * BANK // LIST_ROWS)
+            nc.vector.tensor_copy(x_code[g, half][:], word_table[g][:].indirect(offs_sb[:, columns]))
+
+        def quantize_w1(g, tiles_per_call):
+            dealt = w1_raw[g][:].rearrange("p j (q t r) -> p t q r j", t=PACK, r=BLOCK_ROWS)
+            for call in range(PACK // tiles_per_call):
+                grouped = sb([P, tiles_per_call * P * PACK], BF16, "w1_grouped%d%d" % (g, call))
+                view = grouped[:].rearrange("p (t q r j) -> p t q r j", t=tiles_per_call, r=BLOCK_ROWS, j=PACK)
+                for n in range(tiles_per_call):
+                    nc.scalar.copy(out=view[:, n], in_=dealt[:, tiles_per_call * call + n])
+                columns = slice(tiles_per_call * P * call, tiles_per_call * P * (call + 1))
+                nc.vector.quantize_mx(
+                    out=w1_code[g][:, columns].bitcast(FP8X4), scales=w1_scale[g][:, columns], in_=grouped[:]
+                )
+
+        gather_words(0, 0, behind="")
+        gather_words(0, 1, behind="scale_table")
+        quantize_w1(0, 2)
+        gather_words(1, 0, behind="w1_grouped00")
+        quantize_w1(1, 1)
+        gather_words(1, 1, behind="w1_grouped10")
+
+        w2_raw = sb([P, PACK, N], F32, "w2_raw", tag="word_table0")
+        for t in range(PACK):
+            nc.sync.dma_start(
+                out=w2_raw[:, t, :], in_=w2.rearrange("(q t r) n -> t q r n", t=PACK, r=BLOCK_ROWS)[t]
+            )
 
         h = [sb([P, S], F32, "h%d" % t) for t in range(PACK)]
-        w2_grouped = sb([P, N * PACK], BF16, "w2_grouped")
-        nc.scalar.copy(
-            out=w2_grouped[:].rearrange("p (c i j) -> p c j i", i=4, j=PACK),
-            in_=w2_raw[:].rearrange("p j (c i) -> p c j i", i=4),
-        )
-        for group in ((0, 1, 2), (3,)):
+        for pair in ((0, 1), (2, 3)):
             h_bank = {
-                (t, half): bank(H_BANKS[t] + half, "h_bank%d%d" % (t, half)) for t in group for half in range(2)
+                (t, half): bank(H_BANKS[t] + half, "h_bank%d%d" % (t, half)) for t in pair for half in range(2)
             }
             for g in range(PASSES):
-                for t in group:
+                for t in pair:
                     for half in range(2):
                         nc.tensor.matmul_mx(
                             out=h_bank[t, half][:],
@@ -144,64 +151,69 @@ def tile_picked_lapl_none_p_kernel(
                             start=(g == 0),
                             stop=(g == PASSES - 1),
                         )
-            for t in group:
+            for t in pair:
                 for half in range(2):
-                    dst = h[t][:, BANK * half : BANK * (half + 1)]
+                    place = h[t][:, BANK * half : BANK * (half + 1)]
                     if (t, half) == (0, 1):
-                        nc.vector.tensor_copy(dst, h_bank[t, half][:])
+                        nc.vector.tensor_copy(place, h_bank[t, half][:])
                     else:
-                        nc.scalar.copy(dst, h_bank[t, half][:])
+                        nc.scalar.copy(place, h_bank[t, half][:])
+
+        w2_grouped = sb([P, N * PACK], BF16, "w2_grouped", tag="x_code00")
+        nc.scalar.copy(
+            out=w2_grouped[:].rearrange("p (c i t) -> p c t i", i=4, t=PACK),
+            in_=w2_raw[:].rearrange("p t (c i) -> p c t i", i=4),
+        )
         w2_code = sb([P, N], U32, "w2_code")
         w2_scale = sb([P, N], U8, "w2_scale")
         nc.vector.quantize_mx(out=w2_code[:].bitcast(FP8X4), scales=w2_scale[:], in_=w2_grouped[:])
 
-        gate_bank = bank(6, "gate_bank")
+        gate_bank = bank(GATE_BANK, "gate_bank")
         nc.tensor.transpose(gate_bank[:, 0:P], gate_rows[:], ident[:])
-        neg_gate = sb([P, 8], F32, "neg_gate")
-        nc.scalar.activation(neg_gate[:], gate_bank[:, 0:8], COPY, scale=-1.0)
+        neg_gate = sb([P, 2 * GATE_COLUMNS], F32, "neg_gate")
+        nc.scalar.activation(neg_gate[:], gate_bank[:, 0 : 2 * GATE_COLUMNS], COPY, scale=-1.0)
 
-        blocks = CHUNK // P
-        z_bank = {}
-
-        def turn_neighbours(ci):
-            columns = slice(ci * CHUNK // 16, (ci + 1) * CHUNK // 16)
-            for b in range(blocks):
-                z_bank[ci, b] = bank(Z_BANKS[blocks * ci + b], "z_bank%d%d" % (ci, b))
+        def weighted_sums(chunk):
+            columns = slice(chunk * CHUNK // LIST_ROWS, (chunk + 1) * CHUNK // LIST_ROWS)
+            sums = [bank(SUM_BANKS[BLOCKS * chunk + b], "sum_bank%d%d" % (chunk, b)) for b in range(BLOCKS)]
             for t in range(PACK):
-                stage = bank(STAGE_BANKS[t], "stage%d%d" % (ci, t))
-                for li in range(2):
-                    picked = keep.tile(
-                        [P, CHUNK], F32, name="picked%d%d%d" % (ci, t, li), tag="picked%d" % li, bufs=2, align_bytes=64
-                    )
-                    nc.vector.tensor_copy(picked[:], h[t][:].indirect(lists[li][:, columns]))
-                    for b in range(blocks):
-                        col = CHUNK * li + P * b
+                stage = bank(STAGE_BANKS[t], "stage%d%d" % (chunk, t))
+                for d in range(2):
+                    picked = sb([P, CHUNK], F32, "picked%d%d%d" % (chunk, t, d), tag="picked%d" % d, bufs=2)
+                    nc.vector.tensor_copy(picked[:], h[t][:].indirect(neighbour_lists[d][:, columns]))
+                    for b in range(BLOCKS):
+                        col = CHUNK * d + P * b
                         nc.tensor.transpose(stage[:, col : col + P], picked[:, P * b : P * (b + 1)], ident[:])
-                term = sb([P, 2 * CHUNK], F32, "term%d%d" % (ci, t))
-                for b in range(blocks):
-                    for li in range(2):
-                        col = CHUNK * li + P * b
-                        gcol = 4 * li + blocks * ci + b
+                term = sb([P, 2 * CHUNK], F32, "term%d%d" % (chunk, t))
+                for b in range(BLOCKS):
+                    for d in range(2):
+                        col = CHUNK * d + P * b
+                        gate_col = GATE_COLUMNS * d + BLOCKS * chunk + b
                         nc.scalar.activation(
-                            term[:, col : col + P], stage[:, col : col + P], COPY, scale=neg_gate[:, gcol : gcol + 1]
+                            term[:, col : col + P],
+                            stage[:, col : col + P],
+                            COPY,
+                            scale=neg_gate[:, gate_col : gate_col + 1],
                         )
-                for b in range(blocks):
-                    for li in range(2):
-                        col = CHUNK * li + P * b
+                for b in range(BLOCKS):
+                    for d in range(2):
+                        col = CHUNK * d + P * b
                         nc.tensor.matmul(
-                            z_bank[ci, b][:, P * t : P * (t + 1)],
+                            sums[b][:, P * t : P * (t + 1)],
                             lhsT=term[:, col : col + P],
                             rhs=ident[:],
                             is_transpose=True,
-                            start=(li == 0),
-                            stop=(li == 1),
+                            start=(d == 0),
+                            stop=(d == 1),
                         )
+            return sums
 
-        def gather_centres(ci, centre):
-            columns = slice(ci * CHUNK // 16, (ci + 1) * CHUNK // 16)
+        def gather_centres(chunk, tag):
+            centres = sb([P, PACK * CHUNK], F32, "centres%d" % chunk, tag=tag)
+            columns = slice(chunk * CHUNK // LIST_ROWS, (chunk + 1) * CHUNK // LIST_ROWS)
             for t in range(PACK):
-                nc.vector.tensor_copy(centre[:, CHUNK * t : CHUNK * (t + 1)], h[t][:].indirect(cen_sb[:, columns]))
-            return centre[:].rearrange("p (t v) -> p t v", t=PACK)
+                nc.vector.tensor_copy(centres[:, CHUNK * t : CHUNK * (t + 1)], h[t][:].indirect(cen_sb[:, columns]))
+            return centres[:].rearrange("p (t v) -> p t v", t=PACK)
 
         def project(piece, z_grouped, v0, width):
             z_code = sb([P, width], U32, "z_code%d" % piece)
@@ -218,41 +230,42 @@ def tile_picked_lapl_none_p_kernel(
                     start=True,
                     stop=True,
                 )
-            result = sb([P, 2 * width], F32, "result%d" % piece)
-            nc.scalar.copy(result[:], out_bank[:, 0 : 2 * width])
+            result = sb([P, N // P * width], F32, "result%d" % piece)
+            if piece == len(OUT_BANKS) - 1:
+                nc.vector.tensor_copy(result[:], out_bank[:, 0 : N // P * width])
+            else:
+                nc.scalar.copy(result[:], out_bank[:, 0 : N // P * width])
             nc.sync.dma_start(
                 out=out.rearrange("(a p) v -> p a v", p=P)[:, :, v0 : v0 + width],
-                in_=result[:].rearrange("p (a v) -> p a v", a=2),
+                in_=result[:].rearrange("p (a v) -> p a v", a=N // P),
             )
 
-        turn_neighbours(0)
-        centre_0 = gather_centres(0, sb([P, PACK * CHUNK], F32, "centre0"))
-        z_grouped_0 = keep.tile([P, CHUNK * PACK], BF16, name="z_grouped0", tag="late", align_bytes=64)
-        for b in range(blocks):
-            z_sum = sb([P, BANK], F32, "z_sum%d" % b)
+        sums_0 = weighted_sums(0)
+        centres_0 = gather_centres(0, tag="")
+        z_grouped_0 = sb([P, CHUNK * PACK], BF16, "z_grouped0")
+        for b in range(BLOCKS):
+            z_block = sb([P, PACK * P], F32, "z_block%d" % b)
             nc.vector.tensor_tensor(
-                z_sum[:].rearrange("p (t v) -> p t v", t=PACK),
-                z_bank[0, b][:].rearrange("p (t v) -> p t v", t=PACK),
-                centre_0[:, :, P * b : P * (b + 1)],
+                z_block[:].rearrange("p (t v) -> p t v", t=PACK),
+                sums_0[b][:].rearrange("p (t v) -> p t v", t=PACK),
+                centres_0[:, :, P * b : P * (b + 1)],
                 ADD,
             )
             nc.scalar.copy(
-                out=z_grouped_0[:, BANK * b : BANK * (b + 1)].rearrange("p (v t) -> p v t", t=PACK),
-                in_=z_sum[:].rearrange("p (t v) -> p v t", t=PACK),
+                out=z_grouped_0[:, PACK * P * b : PACK * P * (b + 1)].rearrange("p (v t) -> p v t", t=PACK),
+                in_=z_block[:].rearrange("p (t v) -> p v t", t=PACK),
             )
         project(0, z_grouped_0, 0, CHUNK)
 
-        turn_neighbours(1)
-        centre_1 = gather_centres(
-            1, keep.tile([P, PACK * CHUNK], F32, name="centre1", tag="late", align_bytes=64)
-        )
-        z_grouped_1 = [sb([P, BANK], BF16, "z_grouped1%d" % b) for b in range(blocks)]
-        for b in range(blocks):
+        sums_1 = weighted_sums(1)
+        centres_1 = gather_centres(1, tag="z_grouped0")
+        z_grouped_1 = [sb([P, PACK * P], BF16, "z_grouped1%d" % b) for b in range(BLOCKS)]
+        for b in range(BLOCKS):
             nc.vector.tensor_tensor(
                 z_grouped_1[b][:].rearrange("p (c i t) -> p c t i", i=4, t=PACK),
-                z_bank[1, b][:].rearrange("p (t c i) -> p c t i", i=4, t=PACK),
-                centre_1[:, :, P * b : P * (b + 1)].rearrange("p t (c i) -> p c t i", i=4),
+                sums_1[b][:].rearrange("p (t c i) -> p c t i", i=4, t=PACK),
+                centres_1[:, :, P * b : P * (b + 1)].rearrange("p t (c i) -> p c t i", i=4),
                 ADD,
             )
-        for b in range(blocks):
+        for b in range(BLOCKS):
             project(1 + b, z_grouped_1[b], CHUNK + P * b, P)

@@ -16,6 +16,7 @@ FP8X4 = mybir.dt.float8_e4m3fn_x4
 FP4X4 = mybir.dt.float4_e2m1fn_x4
 COPY = mybir.ActivationFunctionType.Copy
 ADD = mybir.AluOpType.add
+MULT = mybir.AluOpType.mult
 
 P = 128
 PACK = 4
@@ -24,15 +25,13 @@ PASSES = K // (P * PACK)
 QUADRANTS = 4
 BLOCK_ROWS = 8
 LIST_ROWS = 16
-CHUNK = 256
-BLOCKS = CHUNK // P
-GATE_COLUMNS = V // P
+BLOCKS = V // P
 
-H_BANKS = (0, 2, 0, 2)
-GATE_BANK = 4
-STAGE_BANKS = (4, 5, 0, 1)
-SUM_BANKS = (6, 7, 2, 3)
-OUT_BANKS = (6, 7, 4)
+H_BANKS = (0, 0, 2, 0)
+GATE_BANKS = (4, 5)
+TURNED_BANKS = (0, 1, 2, 3)
+BACK_BANKS = (4, 5, 6)
+OUT_BANKS = (1, 0, 2)
 
 
 def tile_picked_lapl_none_p_kernel(
@@ -52,8 +51,6 @@ def tile_picked_lapl_none_p_kernel(
         scale_table = sb([P, T], U8, "scale_table")
         nc.gpsimd.memset(scale_table[:, 0 : T // 2].bitcast(I32), 0)
         nc.vector.memset(scale_table[:, T // 2 : T].bitcast(I32), 0)
-        scales_1 = sb([P, S], U8, "scales_1")
-        nc.vector.memset(scales_1[:].bitcast(I32), 0)
 
         def load_list(name, src):
             tile = keep.tile([P, src.shape[1]], U16, name=name)
@@ -61,72 +58,112 @@ def tile_picked_lapl_none_p_kernel(
             return tile
 
         word_table = [sb([P, T], U16, "word_table%d" % g) for g in range(PASSES)]
-        w1_raw = [sb([P, PACK, H], F32, "w1_raw%d" % g) for g in range(PASSES)]
+        w1_raw = {(g, s): sb([P, PACK, H // 2], F32, "w1_raw%d%d" % (g, s)) for g, s in ((0, 0), (1, 0), (0, 1))}
 
         def load_words(g):
             nc.sync.dma_start(out=word_table[g][:].bitcast(I32), in_=x_words[g].bitcast(I32))
 
-        def load_w1(g):
-            rows = w1[P * PACK * g : P * PACK * (g + 1), :]
-            nc.sync.dma_start(out=w1_raw[g][:], in_=rows.rearrange("(p j) c -> p j c", j=PACK))
+        def load_w1(g, s):
+            rows = w1[P * PACK * g : P * PACK * (g + 1), H // 2 * s : H // 2 * (s + 1)]
+            nc.sync.dma_start(out=w1_raw[g, s][:], in_=rows.rearrange("(p j) c -> p j c", j=PACK))
 
         offs_sb = load_list("offs_sb", offs)
         load_words(0)
+        nc.sync.dma_start(out=scale_table[4:20, :].bitcast(I32), in_=x_scales[1].bitcast(I32))
         for q in range(QUADRANTS):
             nc.sync.dma_start(
-                out=scale_table[32 * q : 32 * q + 4 * PASSES, :].bitcast(I32),
-                in_=x_scales[:, 4 * q : 4 * q + 4, :].bitcast(I32),
+                out=scale_table[32 * q : 32 * q + 4, :].bitcast(I32),
+                in_=x_scales[0, 4 * q : 4 * q + 4, :].bitcast(I32),
             )
-        load_w1(0)
-        load_words(1)
-        load_w1(1)
+        gate_cols = sb([P, 2, BLOCKS], F32, "gate_cols")
+        nc.sync.dma_start(out=gate_cols[:], in_=gate[:, 0, :].rearrange("d (p b) -> p d b", b=BLOCKS))
+        load_w1(0, 0)
+        load_w1(1, 0)
         neighbour_lists = [load_list("pos1_sb", pos1), load_list("pos2_sb", pos2)]
         cen_sb = load_list("cen_sb", cen)
+        load_words(1)
+        load_w1(0, 1)
 
         ident = sb([P, P], F32, "ident")
         make_identity(nc, ident[:])
-        gate_rows = sb([P, P], F32, "gate_rows")
-        nc.gpsimd.memset(gate_rows[:], 0.0)
-        nc.sync.dma_start(
-            out=gate_rows[0 : 2 * GATE_COLUMNS, :], in_=gate[:, 0, :].rearrange("d (b c) -> d b c", c=P)
-        )
+        neg_cols = sb([P, 2 * BLOCKS], F32, "neg_cols")
+        nc.scalar.activation(neg_cols[:], gate_cols[:].rearrange("p d b -> p (d b)"), COPY, scale=-1.0)
 
         scales_0 = sb([P, S], U8, "scales_0")
         nc.vector.tensor_copy(scales_0[:], scale_table[:].indirect(offs_sb[:]))
+        scales_1 = sb([P, S], U8, "scales_1")
+        nc.vector.memset(scales_1[:].bitcast(I32), 0)
         for q in range(QUADRANTS):
             nc.sync.dma_start(
                 out=scales_1[32 * q : 32 * q + 4, :].bitcast(I32),
-                in_=scales_0[32 * q + 4 : 32 * q + 8, :].bitcast(I32),
+                in_=scales_0[4 * q + 4 : 4 * q + 8, :].bitcast(I32),
             )
         x_scale = [scales_0, scales_1]
+        w1_raw[1, 1] = sb([P, PACK, H // 2], F32, "w1_raw11")
+        load_w1(1, 1)
 
         x_code = {}
-        w1_code = [sb([P, H], U32, "w1_code%d" % g) for g in range(PASSES)]
-        w1_scale = [sb([P, H], U8, "w1_scale%d" % g) for g in range(PASSES)]
+        w1_code = {}
+        w1_scale = {}
 
-        def gather_words(g, half, behind):
+        def gather_words(g, half, behind, pieces=1):
             x_code[g, half] = sb([P, BANK], U16, "x_code%d%d" % (g, half), tag=behind)
-            columns = slice(half * BANK // LIST_ROWS, (half + 1) * BANK // LIST_ROWS)
-            nc.vector.tensor_copy(x_code[g, half][:], word_table[g][:].indirect(offs_sb[:, columns]))
-
-        def quantize_w1(g, tiles_per_call):
-            dealt = w1_raw[g][:].rearrange("p j (q t r) -> p t q r j", t=PACK, r=BLOCK_ROWS)
-            for call in range(PACK // tiles_per_call):
-                grouped = sb([P, tiles_per_call * P * PACK], BF16, "w1_grouped%d%d" % (g, call))
-                view = grouped[:].rearrange("p (t q r j) -> p t q r j", t=tiles_per_call, r=BLOCK_ROWS, j=PACK)
-                for n in range(tiles_per_call):
-                    nc.scalar.copy(out=view[:, n], in_=dealt[:, tiles_per_call * call + n])
-                columns = slice(tiles_per_call * P * call, tiles_per_call * P * (call + 1))
-                nc.vector.quantize_mx(
-                    out=w1_code[g][:, columns].bitcast(FP8X4), scales=w1_scale[g][:, columns], in_=grouped[:]
+            width = BANK // pieces
+            for n in range(pieces):
+                first = half * BANK + n * width
+                columns = slice(first // LIST_ROWS, (first + width) // LIST_ROWS)
+                nc.vector.tensor_copy(
+                    x_code[g, half][:, n * width : (n + 1) * width], word_table[g][:].indirect(offs_sb[:, columns])
                 )
 
+        def quantize_w1(g, first, count, grouped, behind=""):
+            code = sb([P, count * P], U32, "w1_code%d%d" % (g, first), tag=behind)
+            scale = sb([P, count * P], U8, "w1_scale%d%d" % (g, first))
+            nc.vector.quantize_mx(out=code[:].bitcast(FP8X4), scales=scale[:], in_=grouped[:])
+            for n in range(count):
+                w1_code[g, first + n] = code[:, P * n : P * (n + 1)]
+                w1_scale[g, first + n] = scale[:, P * n : P * (n + 1)]
+
+        def quantize_low(g, s, behind="", copy=nc.scalar.copy):
+            grouped = sb([P, P * PACK], BF16, "w1_grouped%d%d" % (g, s))
+            copy(
+                out=grouped[:].rearrange("p (q c i j) -> p q c j i", c=4, i=4, j=PACK),
+                in_=w1_raw[g, s][:].rearrange("p j (q c i) -> p q c j i", c=8, i=4)[:, :, 0:4],
+            )
+            quantize_w1(g, s, 1, grouped, behind)
+
+        def quantize_high(g, tiles, behind="", copy_behind=""):
+            grouped = sb([P, len(tiles) * P * PACK], BF16, "w1_grouped%d%d" % (g, tiles[0]), tag=copy_behind)
+            view = grouped[:].rearrange("p (e s q c i j) -> p e s q c j i", e=len(tiles), s=2, c=2, i=4, j=PACK)
+            for e, t in enumerate(tiles):
+                for s in range(2):
+                    dealt = w1_raw[g, s][:].rearrange("p j (q t c i) -> p t q c j i", t=PACK, c=2, i=4)
+                    nc.scalar.copy(out=view[:, e, s], in_=dealt[:, t])
+            quantize_w1(g, tiles[0], len(tiles), grouped, behind)
+
         gather_words(0, 0, behind="")
-        gather_words(0, 1, behind="scale_table")
-        quantize_w1(0, 2)
-        gather_words(1, 0, behind="w1_grouped00")
-        quantize_w1(1, 1)
-        gather_words(1, 1, behind="w1_grouped10")
+        gather_words(0, 1, behind="gate_cols")
+        quantize_low(0, 0)
+        quantize_low(1, 0)
+        gather_words(1, 0, behind="")
+        gather_words(1, 1, behind="", pieces=2)
+        neg_gate = []
+        for d in range(2):
+            spread = bank(GATE_BANKS[d], "spread%d" % d)
+            for b in range(BLOCKS):
+                col = BLOCKS * d + b
+                nc.tensor.transpose(
+                    spread[:, P * b : P * (b + 1)], neg_cols[:, col : col + 1].to_broadcast([P, P]), ident[:]
+                )
+            neg_gate.append(sb([P, V], F32, "neg_gate%d" % d))
+            nc.scalar.copy(
+                out=neg_gate[d][:].rearrange("p (n b) -> p n b", b=BLOCKS),
+                in_=spread[:].rearrange("p (b n) -> p n b", b=BLOCKS),
+            )
+
+        quantize_low(0, 1)
+        quantize_high(0, (2, 3))
+        quantize_low(1, 1, copy=nc.vector.tensor_copy)
 
         w2_raw = sb([P, PACK, N], F32, "w2_raw", tag="word_table0")
         for t in range(PACK):
@@ -135,31 +172,36 @@ def tile_picked_lapl_none_p_kernel(
             )
 
         h = [sb([P, S], F32, "h%d" % t) for t in range(PACK)]
-        for pair in ((0, 1), (2, 3)):
-            h_bank = {
-                (t, half): bank(H_BANKS[t] + half, "h_bank%d%d" % (t, half)) for t in pair for half in range(2)
-            }
-            for g in range(PASSES):
-                for t in pair:
-                    for half in range(2):
-                        nc.tensor.matmul_mx(
-                            out=h_bank[t, half][:],
-                            lhsT=w1_code[g][:, P * t : P * (t + 1)].bitcast(FP8X4),
-                            lhsT_scale=w1_scale[g][:, P * t : P * (t + 1)],
-                            rhs=x_code[g, half][:].bitcast(FP4X4),
-                            rhs_scale=x_scale[g][:, BANK * half : BANK * (half + 1)],
-                            start=(g == 0),
-                            stop=(g == PASSES - 1),
-                        )
-            for t in pair:
-                for half in range(2):
-                    place = h[t][:, BANK * half : BANK * (half + 1)]
-                    if (t, half) == (0, 1):
-                        nc.vector.tensor_copy(place, h_bank[t, half][:])
-                    else:
-                        nc.scalar.copy(place, h_bank[t, half][:])
 
-        w2_grouped = sb([P, N * PACK], BF16, "w2_grouped", tag="x_code00")
+        def first_product(target, g, t, j0, width):
+            half, start = divmod(j0, BANK)
+            nc.tensor.matmul_mx(
+                out=target,
+                lhsT=w1_code[g, t].bitcast(FP8X4),
+                lhsT_scale=w1_scale[g, t],
+                rhs=x_code[g, half][:, start : start + width].bitcast(FP4X4),
+                rhs_scale=x_scale[g][:, j0 : j0 + width],
+                start=(g == 0),
+                stop=(g == PASSES - 1),
+            )
+
+        for number, j0, width, group in ((0, 0, BANK, BANK), (1, 512, 256, P), (2, 768, P, P), (3, 896, P, P)):
+            target = bank(number, "h_bank0_%d" % number)
+            for start in range(0, width, group):
+                for g in range(PASSES):
+                    first_product(target[:, start : start + group], g, 0, j0 + start, group)
+            nc.scalar.copy(h[0][:, j0 : j0 + width], target[:, 0:width])
+        quantize_high(1, (2,), copy_behind="w1_code10")
+        quantize_high(1, (3,), copy_behind="w1_scale10")
+        for t in range(1, PACK):
+            targets = [bank(H_BANKS[t] + half, "h_bank%d%d" % (t, half)) for half in range(2)]
+            for g in range(PASSES):
+                for half in range(2):
+                    first_product(targets[half][:], g, t, BANK * half, BANK)
+            for half in range(2):
+                nc.scalar.copy(h[t][:, BANK * half : BANK * (half + 1)], targets[half][:])
+
+        w2_grouped = sb([P, N * PACK], BF16, "w2_grouped", tag="x_code11")
         nc.scalar.copy(
             out=w2_grouped[:].rearrange("p (c i t) -> p c t i", i=4, t=PACK),
             in_=w2_raw[:].rearrange("p t (c i) -> p c t i", i=4),
@@ -168,57 +210,64 @@ def tile_picked_lapl_none_p_kernel(
         w2_scale = sb([P, N], U8, "w2_scale")
         nc.vector.quantize_mx(out=w2_code[:].bitcast(FP8X4), scales=w2_scale[:], in_=w2_grouped[:])
 
-        gate_bank = bank(GATE_BANK, "gate_bank")
-        nc.tensor.transpose(gate_bank[:, 0:P], gate_rows[:], ident[:])
-        neg_gate = sb([P, 2 * GATE_COLUMNS], F32, "neg_gate")
-        nc.scalar.activation(neg_gate[:], gate_bank[:, 0 : 2 * GATE_COLUMNS], COPY, scale=-1.0)
+        turned = {}
+        for b in range(BLOCKS):
+            turned[b, 0] = turned[b, 1] = bank(TURNED_BANKS[b], "turned%d" % b)
+        rows = [sb([P, H], BF16, "rows%d" % b) for b in range(BLOCKS)]
 
-        def weighted_sums(chunk):
-            columns = slice(chunk * CHUNK // LIST_ROWS, (chunk + 1) * CHUNK // LIST_ROWS)
-            sums = [bank(SUM_BANKS[BLOCKS * chunk + b], "sum_bank%d%d" % (chunk, b)) for b in range(BLOCKS)]
-            for t in range(PACK):
-                stage = bank(STAGE_BANKS[t], "stage%d%d" % (chunk, t))
+        def gather_terms(tiles, v0, width, behind="", tags=("near", "far"), bufs=2):
+            name = "%d_%d" % (tiles[0], v0)
+            columns = slice(v0 // LIST_ROWS, (v0 + width) // LIST_ROWS)
+            products = [
+                sb([P, len(tiles), width], F32, "products%d_%s" % (d, name), tag=tags[d], bufs=bufs) for d in range(2)
+            ]
+            first = sb([P, len(tiles), width], F32, "first" + name, tag=behind)
+            for n, t in enumerate(tiles):
                 for d in range(2):
-                    picked = sb([P, CHUNK], F32, "picked%d%d%d" % (chunk, t, d), tag="picked%d" % d, bufs=2)
-                    nc.vector.tensor_copy(picked[:], h[t][:].indirect(neighbour_lists[d][:, columns]))
-                    for b in range(BLOCKS):
-                        col = CHUNK * d + P * b
-                        nc.tensor.transpose(stage[:, col : col + P], picked[:, P * b : P * (b + 1)], ident[:])
-                term = sb([P, 2 * CHUNK], F32, "term%d%d" % (chunk, t))
-                for b in range(BLOCKS):
-                    for d in range(2):
-                        col = CHUNK * d + P * b
-                        gate_col = GATE_COLUMNS * d + BLOCKS * chunk + b
-                        nc.scalar.activation(
-                            term[:, col : col + P],
-                            stage[:, col : col + P],
-                            COPY,
-                            scale=neg_gate[:, gate_col : gate_col + 1],
-                        )
-                for b in range(BLOCKS):
-                    for d in range(2):
-                        col = CHUNK * d + P * b
+                    nc.vector.tensor_tensor(
+                        products[d][:, n, :],
+                        h[t][:].indirect(neighbour_lists[d][:, columns]),
+                        neg_gate[d][:, v0 : v0 + width],
+                        MULT,
+                    )
+            for n, t in enumerate(tiles):
+                nc.vector.tensor_tensor(first[:, n, :], h[t][:].indirect(cen_sb[:, columns]), products[0][:, n, :], ADD)
+            return first, products[1]
+
+        def add_turned(tiles, v0, width, behind="", tags=("near", "far"), bufs=2):
+            first, second = gather_terms(tiles, v0, width, behind, tags, bufs)
+            for n, t in enumerate(tiles):
+                for b in range(v0 // P, (v0 + width) // P):
+                    cols = slice(P * b - v0, P * (b + 1) - v0)
+                    for term, start in ((second, True), (first, False)):
                         nc.tensor.matmul(
-                            sums[b][:, P * t : P * (t + 1)],
-                            lhsT=term[:, col : col + P],
+                            turned[b, t // 2][:, P * t : P * (t + 1)],
+                            lhsT=term[:, n, cols],
                             rhs=ident[:],
                             is_transpose=True,
-                            start=(d == 0),
-                            stop=(d == 1),
+                            start=start,
+                            stop=not start,
                         )
-            return sums
 
-        def gather_centres(chunk, tag):
-            centres = sb([P, PACK * CHUNK], F32, "centres%d" % chunk, tag=tag)
-            columns = slice(chunk * CHUNK // LIST_ROWS, (chunk + 1) * CHUNK // LIST_ROWS)
-            for t in range(PACK):
-                nc.vector.tensor_copy(centres[:, CHUNK * t : CHUNK * (t + 1)], h[t][:].indirect(cen_sb[:, columns]))
-            return centres[:].rearrange("p (t v) -> p t v", t=PACK)
+        def round_pair(b, u):
+            cols = slice(2 * P * u, 2 * P * (u + 1))
+            run = BLOCK_ROWS if u == 0 else P
+            nc.scalar.copy(
+                out=rows[b][:, cols].rearrange("v (q r e) -> v q r e", r=run, e=2),
+                in_=turned[b, u][:, cols].rearrange("v (q e r) -> v q r e", r=run, e=2),
+            )
+
+        def turn_back(back, place, b, u):
+            nc.tensor.transpose(
+                back[:, P * place : P * (place + 1)], rows[b][:].bitcast(F32)[:, P * u : P * (u + 1)], ident[:]
+            )
 
         def project(piece, z_grouped, v0, width):
-            z_code = sb([P, width], U32, "z_code%d" % piece)
+            z_code = sb([P, width], U32, "z_code%d" % piece, tag="z_grouped2" if piece == 2 else "")
             z_scale = sb([P, width], U8, "z_scale%d" % piece)
-            nc.vector.quantize_mx(out=z_code[:].bitcast(FP8X4), scales=z_scale[:], in_=z_grouped[:])
+            for n, block in enumerate(z_grouped):
+                cols = slice(P * n, P * (n + 1))
+                nc.vector.quantize_mx(out=z_code[:, cols].bitcast(FP8X4), scales=z_scale[:, cols], in_=block[:])
             out_bank = bank(OUT_BANKS[piece], "out_bank%d" % piece)
             for a in range(N // P):
                 nc.tensor.matmul_mx(
@@ -240,32 +289,43 @@ def tile_picked_lapl_none_p_kernel(
                 in_=result[:].rearrange("p (a v) -> p a v", a=N // P),
             )
 
-        sums_0 = weighted_sums(0)
-        centres_0 = gather_centres(0, tag="")
-        z_grouped_0 = sb([P, CHUNK * PACK], BF16, "z_grouped0")
-        for b in range(BLOCKS):
-            z_block = sb([P, PACK * P], F32, "z_block%d" % b)
-            nc.vector.tensor_tensor(
-                z_block[:].rearrange("p (t v) -> p t v", t=PACK),
-                sums_0[b][:].rearrange("p (t v) -> p t v", t=PACK),
-                centres_0[:, :, P * b : P * (b + 1)],
-                ADD,
-            )
+        def finish_turned(b):
+            back = bank(BACK_BANKS[b], "back%d" % b)
+            round_pair(b, 1)
+            for u in range(2):
+                turn_back(back, u, b, u)
+            z_grouped = sb([P, P * PACK], BF16, "z_grouped%d" % b)
             nc.scalar.copy(
-                out=z_grouped_0[:, PACK * P * b : PACK * P * (b + 1)].rearrange("p (v t) -> p v t", t=PACK),
-                in_=z_block[:].rearrange("p (t v) -> p v t", t=PACK),
+                out=z_grouped[:].bitcast(F32).rearrange("p (v u) -> p v u", u=2),
+                in_=back[:, 0 : 2 * P].rearrange("p (u v) -> p v u", u=2),
             )
-        project(0, z_grouped_0, 0, CHUNK)
+            return z_grouped
 
-        sums_1 = weighted_sums(1)
-        centres_1 = gather_centres(1, tag="z_grouped0")
-        z_grouped_1 = [sb([P, PACK * P], BF16, "z_grouped1%d" % b) for b in range(BLOCKS)]
+        add_turned((0,), 0, V, tags=("", "w1_grouped11"), bufs=1)
+        add_turned((1,), 0, V, tags=("w1_code10", "w1_scale10"), bufs=1)
         for b in range(BLOCKS):
-            nc.vector.tensor_tensor(
-                z_grouped_1[b][:].rearrange("p (c i t) -> p c t i", i=4, t=PACK),
-                sums_1[b][:].rearrange("p (t c i) -> p c t i", i=4, t=PACK),
-                centres_1[:, :, P * b : P * (b + 1)].rearrange("p t (c i) -> p c t i", i=4),
-                ADD,
-            )
-        for b in range(BLOCKS):
-            project(1 + b, z_grouped_1[b], CHUNK + P * b, P)
+            round_pair(b, 0)
+        last = BLOCKS - 1
+        back_last = bank(BACK_BANKS[2], "back_last")
+        turn_back(back_last, 0, last, 0)
+        z_last = sb([P, P * PACK], BF16, "z_last")
+        nc.scalar.copy(
+            out=z_last[:].bitcast(F32).rearrange("p (v u) -> p v u", u=2)[:, :, 0], in_=back_last[:, 0:P]
+        )
+
+        add_turned((2,), 0, 2 * P)
+        add_turned((3,), 0, 2 * P)
+        z_0 = [finish_turned(0), finish_turned(1)]
+        turned[2, 1] = bank(TURNED_BANKS[1], "turned_late")
+        add_turned((2, 3), 2 * P, P)
+        z_1 = [finish_turned(2)]
+        project(0, z_0, 0, 2 * P)
+        first, second = gather_terms((2, 3), P * last, P, behind="z_grouped0")
+        nc.vector.tensor_tensor(
+            z_last[:].rearrange("p (v u e) -> p v u e", u=2, e=2)[:, :, 1, :],
+            first[:].rearrange("p e v -> p v e"),
+            second[:].rearrange("p e v -> p v e"),
+            ADD,
+        )
+        project(1, z_1, 2 * P, P)
+        project(2, [z_last], P * last, P)

@@ -40,12 +40,15 @@ def tile_picked_lapl_none_p_kernel(
     nc = tc.nc
     with ExitStack() as ctx:
         keep = ctx.enter_context(tc.tile_pool(name="keep", bufs=1))
+        shared = ctx.enter_context(tc.tile_pool(name="shared", bufs=1))
         psum = ctx.enter_context(tc.psum_pool(name="psum", bufs=1))
 
         def bank(number, name):
             return psum.tile([P, BANK], F32, name=name, tag="bank%d" % number)
 
         def sb(shape, dtype, name, tag="", bufs=1):
+            if isinstance(tag, int):
+                return shared.tile(shape, dtype, name=name, align_bytes=64, offset=tag)
             return keep.tile(shape, dtype, name=name, tag=tag or name, bufs=bufs, align_bytes=64)
 
         scale_table = sb([P, T], U8, "scale_table")
@@ -57,7 +60,7 @@ def tile_picked_lapl_none_p_kernel(
             nc.sync.dma_start(tile[:], src)
             return tile
 
-        word_table = [sb([P, T], U16, "word_table%d" % g) for g in range(PASSES)]
+        word_table = [sb([P, T], U16, "word_table0", tag=24576), sb([P, T], U16, "word_table1")]
         w1_raw = {(g, s): sb([P, PACK, H // 2], F32, "w1_raw%d%d" % (g, s)) for g, s in ((0, 0), (1, 0), (0, 1))}
 
         def load_words(g):
@@ -165,7 +168,7 @@ def tile_picked_lapl_none_p_kernel(
         quantize_high(0, (2, 3))
         quantize_low(1, 1, copy=nc.vector.tensor_copy)
 
-        w2_raw = sb([P, PACK, N], F32, "w2_raw", tag="word_table0")
+        w2_raw = sb([P, PACK, N], F32, "w2_raw", tag=24576)
         for t in range(PACK):
             nc.sync.dma_start(
                 out=w2_raw[:, t, :], in_=w2.rearrange("(q t r) n -> t q r n", t=PACK, r=BLOCK_ROWS)[t]
@@ -213,17 +216,20 @@ def tile_picked_lapl_none_p_kernel(
         turned = {}
         for b in range(BLOCKS):
             turned[b, 0] = turned[b, 1] = bank(TURNED_BANKS[b], "turned%d" % b)
-        rows = [sb([P, H], BF16, "rows%d" % b) for b in range(BLOCKS)]
+        rows = [sb([P, H], BF16, "rows%d" % b, tag=28672 if b == 1 else "") for b in range(BLOCKS)]
 
-        def gather_terms(tiles, v0, width, behind="", tags=("near", "far"), bufs=2):
+        def gather_terms(tiles, v0, width, behind="", tags=("", ""), bufs=1, order=(0, 1)):
             name = "%d_%d" % (tiles[0], v0)
             columns = slice(v0 // LIST_ROWS, (v0 + width) // LIST_ROWS)
             products = [
                 sb([P, len(tiles), width], F32, "products%d_%s" % (d, name), tag=tags[d], bufs=bufs) for d in range(2)
             ]
             first = sb([P, len(tiles), width], F32, "first" + name, tag=behind)
-            for n, t in enumerate(tiles):
-                for d in range(2):
+            steps = [(n, t, d) for n, t in enumerate(tiles) for d in range(2)]
+            if order != (0, 1):
+                steps = [(n, t, d) for d in order for n, t in enumerate(tiles)]
+            for n, t, d in steps:
+                if True:
                     nc.vector.tensor_tensor(
                         products[d][:, n, :],
                         h[t][:].indirect(neighbour_lists[d][:, columns]),
@@ -234,7 +240,7 @@ def tile_picked_lapl_none_p_kernel(
                 nc.vector.tensor_tensor(first[:, n, :], h[t][:].indirect(cen_sb[:, columns]), products[0][:, n, :], ADD)
             return first, products[1]
 
-        def add_turned(tiles, v0, width, behind="", tags=("near", "far"), bufs=2):
+        def add_turned(tiles, v0, width, behind="", tags=("", ""), bufs=1):
             first, second = gather_terms(tiles, v0, width, behind, tags, bufs)
             for n, t in enumerate(tiles):
                 for b in range(v0 // P, (v0 + width) // P):
@@ -263,7 +269,7 @@ def tile_picked_lapl_none_p_kernel(
             )
 
         def project(piece, z_grouped, v0, width):
-            z_code = sb([P, width], U32, "z_code%d" % piece, tag="z_grouped2" if piece == 2 else "")
+            z_code = sb([P, width], U32, "z_code%d" % piece)
             z_scale = sb([P, width], U8, "z_scale%d" % piece)
             for n, block in enumerate(z_grouped):
                 cols = slice(P * n, P * (n + 1))
@@ -317,15 +323,15 @@ def tile_picked_lapl_none_p_kernel(
         add_turned((3,), 0, 2 * P)
         z_0 = [finish_turned(0), finish_turned(1)]
         turned[2, 1] = bank(TURNED_BANKS[1], "turned_late")
-        add_turned((2, 3), 2 * P, P)
+        add_turned((2, 3), 2 * P, P, tags=(24576, 25600))
         z_1 = [finish_turned(2)]
         project(0, z_0, 0, 2 * P)
-        first, second = gather_terms((2, 3), P * last, P, behind="z_grouped0")
+        first, second = gather_terms((2, 3), P * last, P, tags=(28160, 26624), order=(1, 0))
         nc.vector.tensor_tensor(
             z_last[:].rearrange("p (v u e) -> p v u e", u=2, e=2)[:, :, 1, :],
             first[:].rearrange("p e v -> p v e"),
             second[:].rearrange("p e v -> p v e"),
             ADD,
         )
-        project(1, z_1, 2 * P, P)
         project(2, [z_last], P * last, P)
+        project(1, z_1, 2 * P, P)

@@ -31,7 +31,7 @@ H_BANKS = (0, 0, 2, 0)
 GATE_BANKS = (4, 5)
 TURNED_BANKS = (0, 1, 2, 3)
 BACK_BANKS = (4, 5, 6)
-OUT_BANKS = (1, 0, 2)
+OUT_BANKS = (1, 2, 0)
 
 
 def tile_picked_lapl_none_p_kernel(
@@ -268,8 +268,8 @@ def tile_picked_lapl_none_p_kernel(
                 back[:, P * place : P * (place + 1)], rows[b][:].bitcast(F32)[:, P * u : P * (u + 1)], ident[:]
             )
 
-        def project(piece, z_grouped, v0, width):
-            z_code = sb([P, width], U32, "z_code%d" % piece)
+        def project(piece, z_grouped, v0, width, behind=""):
+            z_code = sb([P, width], U32, "z_code%d" % piece, tag=behind)
             z_scale = sb([P, width], U8, "z_scale%d" % piece)
             for n, block in enumerate(z_grouped):
                 cols = slice(P * n, P * (n + 1))
@@ -333,5 +333,5 @@ def tile_picked_lapl_none_p_kernel(
             second[:].rearrange("p e v -> p v e"),
             ADD,
         )
-        project(2, [z_last], P * last, P)
         project(1, z_1, 2 * P, P)
+        project(2, [z_last], P * last, P, behind="z_grouped2")

@@ -120,7 +120,7 @@ def tile_picked_lapl_none_p_kernel(
                 )
 
         def quantize_w1(g, first, count, grouped, behind=""):
-            code = sb([P, count * P], U32, "w1_code%d%d" % (g, first), tag=behind)
+            code = sb([P, count * P], U32, "w1_code%d%d" % (g, first), tag=20480 if (g, first) == (1, 0) else "")
             scale = sb([P, count * P], U8, "w1_scale%d%d" % (g, first))
             nc.vector.quantize_mx(out=code[:].bitcast(FP8X4), scales=scale[:], in_=grouped[:])
             for n in range(count):
@@ -128,21 +128,25 @@ def tile_picked_lapl_none_p_kernel(
                 w1_scale[g, first + n] = scale[:, P * n : P * (n + 1)]
 
         def quantize_low(g, s, behind="", copy=nc.scalar.copy):
-            grouped = sb([P, P * PACK], BF16, "w1_grouped%d%d" % (g, s))
+            grouped = sb([P, P * PACK], BF16, "w1_grouped%d%d" % (g, s), tag=behind)
             copy(
                 out=grouped[:].rearrange("p (q c i j) -> p q c j i", c=4, i=4, j=PACK),
                 in_=w1_raw[g, s][:].rearrange("p j (q c i) -> p q c j i", c=8, i=4)[:, :, 0:4],
             )
             quantize_w1(g, s, 1, grouped, behind)
 
-        def quantize_high(g, tiles, behind="", copy_behind=""):
+        def quantize_high(g, tiles, behind="", copy_behind="", apart=False):
             grouped = sb([P, len(tiles) * P * PACK], BF16, "w1_grouped%d%d" % (g, tiles[0]), tag=copy_behind)
             view = grouped[:].rearrange("p (e s q c i j) -> p e s q c j i", e=len(tiles), s=2, c=2, i=4, j=PACK)
             for e, t in enumerate(tiles):
                 for s in range(2):
                     dealt = w1_raw[g, s][:].rearrange("p j (q t c i) -> p t q c j i", t=PACK, c=2, i=4)
-                    nc.scalar.copy(out=view[:, e, s], in_=dealt[:, t])
-            quantize_w1(g, tiles[0], len(tiles), grouped, behind)
+                    copy = nc.vector.tensor_copy if (g, t, s) == (1, 2, 0) else nc.scalar.copy
+                    copy(out=view[:, e, s], in_=dealt[:, t])
+                if apart:
+                    quantize_w1(g, t, 1, grouped[:, P * PACK * e : P * PACK * (e + 1)])
+            if not apart:
+                quantize_w1(g, tiles[0], len(tiles), grouped, behind)
 
         gather_words(0, 0, behind="")
         gather_words(0, 1, behind="gate_cols")
@@ -166,7 +170,6 @@ def tile_picked_lapl_none_p_kernel(
 
         quantize_low(0, 1)
         quantize_high(0, (2, 3))
-        quantize_low(1, 1, copy=nc.vector.tensor_copy)
 
         w2_raw = sb([P, PACK, N], F32, "w2_raw", tag=24576)
         for t in range(PACK):
@@ -193,9 +196,10 @@ def tile_picked_lapl_none_p_kernel(
             for start in range(0, width, group):
                 for g in range(PASSES):
                     first_product(target[:, start : start + group], g, 0, j0 + start, group)
-            nc.scalar.copy(h[0][:, j0 : j0 + width], target[:, 0:width])
-        quantize_high(1, (2,), copy_behind="w1_code10")
-        quantize_high(1, (3,), copy_behind="w1_scale10")
+            copy = nc.vector.tensor_copy if number == 1 else nc.scalar.copy
+            copy(h[0][:, j0 : j0 + width], target[:, 0:width])
+        quantize_low(1, 1, behind=19712)
+        quantize_high(1, (2, 3), copy_behind="w1_scale10", apart=True)
         for t in range(1, PACK):
             targets = [bank(H_BANKS[t] + half, "h_bank%d%d" % (t, half)) for half in range(2)]
             for g in range(PASSES):
@@ -307,8 +311,8 @@ def tile_picked_lapl_none_p_kernel(
             )
             return z_grouped
 
-        add_turned((0,), 0, V, tags=("", "w1_grouped11"), bufs=1)
-        add_turned((1,), 0, V, tags=("w1_code10", "w1_scale10"), bufs=1)
+        add_turned((0,), 0, V, behind=17728, tags=("", 19776), bufs=1)
+        add_turned((1,), 0, V)
         for b in range(BLOCKS):
             round_pair(b, 0)
         last = BLOCKS - 1

@@ -27,11 +27,11 @@ BLOCK_ROWS = 8
 LIST_ROWS = 16
 BLOCKS = V // P
 
-H_BANKS = (0, 0, 2, 0)
 GATE_BANKS = (4, 5)
-TURNED_BANKS = (0, 1, 2, 3)
-BACK_BANKS = (4, 5, 6)
-OUT_BANKS = (1, 2, 0)
+H_BANKS = (0, 0, 2, 0)
+TURNED_BANKS = ((4, 5), (6, 7))
+BACK_BANKS = (0, 1, 2)
+OUT_BANKS = (3, 4, 5)
 
 
 def tile_picked_lapl_none_p_kernel(
@@ -46,10 +46,10 @@ def tile_picked_lapl_none_p_kernel(
         def bank(number, name):
             return psum.tile([P, BANK], F32, name=name, tag="bank%d" % number)
 
-        def sb(shape, dtype, name, tag="", bufs=1):
+        def sb(shape, dtype, name, tag=""):
             if isinstance(tag, int):
                 return shared.tile(shape, dtype, name=name, align_bytes=64, offset=tag)
-            return keep.tile(shape, dtype, name=name, tag=tag or name, bufs=bufs, align_bytes=64)
+            return keep.tile(shape, dtype, name=name, tag=tag or name, align_bytes=64)
 
         scale_table = sb([P, T], U8, "scale_table")
         nc.gpsimd.memset(scale_table[:, 0 : T // 2].bitcast(I32), 0)
@@ -60,15 +60,19 @@ def tile_picked_lapl_none_p_kernel(
             nc.sync.dma_start(tile[:], src)
             return tile
 
-        word_table = [sb([P, T], U16, "word_table0", tag=24576), sb([P, T], U16, "word_table1")]
-        w1_raw = {(g, s): sb([P, PACK, H // 2], F32, "w1_raw%d%d" % (g, s)) for g, s in ((0, 0), (1, 0), (0, 1))}
+        word_table = [sb([P, T], U16, "word_table%d" % g) for g in range(PASSES)]
+        w1_raw = {}
 
         def load_words(g):
             nc.sync.dma_start(out=word_table[g][:].bitcast(I32), in_=x_words[g].bitcast(I32))
 
-        def load_w1(g, s):
-            rows = w1[P * PACK * g : P * PACK * (g + 1), H // 2 * s : H // 2 * (s + 1)]
-            nc.sync.dma_start(out=w1_raw[g, s][:], in_=rows.rearrange("(p j) c -> p j c", j=PACK))
+        def load_w1(g, halves, behind=""):
+            width = H // 2 * len(halves)
+            raw = sb([P, PACK, width], F32, "w1_raw%d%d" % (g, halves[0]), tag=behind)
+            rows = w1[P * PACK * g : P * PACK * (g + 1), H // 2 * halves[0] : H // 2 * halves[0] + width]
+            nc.sync.dma_start(out=raw[:], in_=rows.rearrange("(p j) c -> p j c", j=PACK))
+            for n, s in enumerate(halves):
+                w1_raw[g, s] = raw[:, :, H // 2 * n : H // 2 * (n + 1)]
 
         offs_sb = load_list("offs_sb", offs)
         load_words(0)
@@ -80,12 +84,12 @@ def tile_picked_lapl_none_p_kernel(
             )
         gate_cols = sb([P, 2, BLOCKS], F32, "gate_cols")
         nc.sync.dma_start(out=gate_cols[:], in_=gate[:, 0, :].rearrange("d (p b) -> p d b", b=BLOCKS))
-        load_w1(0, 0)
-        load_w1(1, 0)
+        load_w1(0, (0,))
+        load_w1(1, (0,))
         neighbour_lists = [load_list("pos1_sb", pos1), load_list("pos2_sb", pos2)]
         cen_sb = load_list("cen_sb", cen)
         load_words(1)
-        load_w1(0, 1)
+        load_w1(0, (1,))
 
         ident = sb([P, P], F32, "ident")
         make_identity(nc, ident[:])
@@ -102,58 +106,46 @@ def tile_picked_lapl_none_p_kernel(
                 in_=scales_0[4 * q + 4 : 4 * q + 8, :].bitcast(I32),
             )
         x_scale = [scales_0, scales_1]
-        w1_raw[1, 1] = sb([P, PACK, H // 2], F32, "w1_raw11")
-        load_w1(1, 1)
+        load_w1(1, (1,), behind="scale_table")
+        w2_raw = sb([P, PACK, N], F32, "w2_raw", tag="word_table0")
+        for t in range(PACK):
+            nc.sync.dma_start(
+                out=w2_raw[:, t, :], in_=w2.rearrange("(q t r) n -> t q r n", t=PACK, r=BLOCK_ROWS)[t]
+            )
 
         x_code = {}
         w1_code = {}
         w1_scale = {}
 
-        def gather_words(g, half, behind, pieces=1):
-            x_code[g, half] = sb([P, BANK], U16, "x_code%d%d" % (g, half), tag=behind)
-            width = BANK // pieces
-            for n in range(pieces):
-                first = half * BANK + n * width
-                columns = slice(first // LIST_ROWS, (first + width) // LIST_ROWS)
-                nc.vector.tensor_copy(
-                    x_code[g, half][:, n * width : (n + 1) * width], word_table[g][:].indirect(offs_sb[:, columns])
-                )
-
-        def quantize_w1(g, first, count, grouped, behind=""):
-            code = sb([P, count * P], U32, "w1_code%d%d" % (g, first), tag=20480 if (g, first) == (1, 0) else "")
-            scale = sb([P, count * P], U8, "w1_scale%d%d" % (g, first))
-            nc.vector.quantize_mx(out=code[:].bitcast(FP8X4), scales=scale[:], in_=grouped[:])
-            for n in range(count):
-                w1_code[g, first + n] = code[:, P * n : P * (n + 1)]
-                w1_scale[g, first + n] = scale[:, P * n : P * (n + 1)]
-
-        def quantize_low(g, s, behind="", copy=nc.scalar.copy):
-            grouped = sb([P, P * PACK], BF16, "w1_grouped%d%d" % (g, s), tag=behind)
-            copy(
-                out=grouped[:].rearrange("p (q c i j) -> p q c j i", c=4, i=4, j=PACK),
-                in_=w1_raw[g, s][:].rearrange("p j (q c i) -> p q c j i", c=8, i=4)[:, :, 0:4],
+        def gather_words(g, half, first, width, behind=""):
+            if first == 0:
+                x_code[g, half] = sb([P, BANK], U16, "x_code%d%d" % (g, half), tag=behind)
+            start = half * BANK + first
+            columns = slice(start // LIST_ROWS, (start + width) // LIST_ROWS)
+            nc.vector.tensor_copy(
+                x_code[g, half][:, first : first + width], word_table[g][:].indirect(offs_sb[:, columns])
             )
-            quantize_w1(g, s, 1, grouped, behind)
 
-        def quantize_high(g, tiles, behind="", copy_behind="", apart=False):
-            grouped = sb([P, len(tiles) * P * PACK], BF16, "w1_grouped%d%d" % (g, tiles[0]), tag=copy_behind)
-            view = grouped[:].rearrange("p (e s q c i j) -> p e s q c j i", e=len(tiles), s=2, c=2, i=4, j=PACK)
+        def round_low(g, s, grouped, copy):
+            copy(
+                out=grouped.rearrange("p (q c i j) -> p q c j i", c=4, i=4, j=PACK),
+                in_=w1_raw[g, s].rearrange("p j (q c i) -> p q c j i", c=8, i=4)[:, :, 0:4],
+            )
+
+        def round_high(g, s, grouped, copy):
+            view = grouped.rearrange("p (e s q c i j) -> p e s q c j i", e=2, s=2, c=2, i=4, j=PACK)
+            dealt = w1_raw[g, s].rearrange("p j (q t c i) -> p t q c j i", t=PACK, c=2, i=4)
+            for e in range(2):
+                copy(out=view[:, e, s], in_=dealt[:, 2 + e])
+
+        def quantize_w1(g, tiles, grouped, behind=""):
+            code = sb([P, len(tiles) * P], U32, "w1_code%d%d" % (g, tiles[0]), tag=behind)
+            scale = sb([P, len(tiles) * P], U8, "w1_scale%d%d" % (g, tiles[0]))
+            nc.vector.quantize_mx(out=code[:].bitcast(FP8X4), scales=scale[:], in_=grouped)
             for e, t in enumerate(tiles):
-                for s in range(2):
-                    dealt = w1_raw[g, s][:].rearrange("p j (q t c i) -> p t q c j i", t=PACK, c=2, i=4)
-                    copy = nc.vector.tensor_copy if (g, t, s) == (1, 2, 0) else nc.scalar.copy
-                    copy(out=view[:, e, s], in_=dealt[:, t])
-                if apart:
-                    quantize_w1(g, t, 1, grouped[:, P * PACK * e : P * PACK * (e + 1)])
-            if not apart:
-                quantize_w1(g, tiles[0], len(tiles), grouped, behind)
+                w1_code[g, t] = code[:, P * e : P * (e + 1)]
+                w1_scale[g, t] = scale[:, P * e : P * (e + 1)]
 
-        gather_words(0, 0, behind="")
-        gather_words(0, 1, behind="gate_cols")
-        quantize_low(0, 0)
-        quantize_low(1, 0)
-        gather_words(1, 0, behind="")
-        gather_words(1, 1, behind="", pieces=2)
         neg_gate = []
         for d in range(2):
             spread = bank(GATE_BANKS[d], "spread%d" % d)
@@ -168,14 +160,28 @@ def tile_picked_lapl_none_p_kernel(
                 in_=spread[:].rearrange("p (b n) -> p n b", b=BLOCKS),
             )
 
-        quantize_low(0, 1)
-        quantize_high(0, (2, 3))
-
-        w2_raw = sb([P, PACK, N], F32, "w2_raw", tag=24576)
-        for t in range(PACK):
-            nc.sync.dma_start(
-                out=w2_raw[:, t, :], in_=w2.rearrange("(q t r) n -> t q r n", t=PACK, r=BLOCK_ROWS)[t]
-            )
+        wide = P * PACK
+        grouped = {
+            (g, t): sb([P, n * wide], BF16, "w1_grouped%d%d" % (g, t))
+            for g, t, n in ((0, 0, 1), (1, 0, 1), (0, 1, 3), (1, 1, 1), (1, 2, 2))
+        }
+        gather_words(0, 0, 0, BANK)
+        gather_words(0, 1, 0, BANK, behind="gate_cols")
+        for g in range(PASSES):
+            round_low(g, 0, grouped[g, 0][:], nc.scalar.copy)
+            quantize_w1(g, (0,), grouped[g, 0][:])
+        round_high(0, 0, grouped[0, 1][:, wide : 3 * wide], nc.scalar.copy)
+        round_high(1, 0, grouped[1, 2][:], nc.scalar.copy)
+        round_low(0, 1, grouped[0, 1][:, 0:wide], nc.scalar.copy)
+        round_high(0, 1, grouped[0, 1][:, wide : 3 * wide], nc.scalar.copy)
+        gather_words(1, 0, 0, BANK)
+        gather_words(1, 1, 0, BANK // 2)
+        gather_words(1, 1, BANK // 2, BANK // 2)
+        quantize_w1(0, (1, 2, 3), grouped[0, 1][:], behind="word_table1")
+        round_low(1, 1, grouped[1, 1][:], nc.vector.tensor_copy)
+        round_high(1, 1, grouped[1, 2][:], nc.vector.tensor_copy)
+        quantize_w1(1, (1,), grouped[1, 1][:])
+        quantize_w1(1, (2, 3), grouped[1, 2][:])
 
         h = [sb([P, S], F32, "h%d" % t) for t in range(PACK)]
 
@@ -191,93 +197,92 @@ def tile_picked_lapl_none_p_kernel(
                 stop=(g == PASSES - 1),
             )
 
-        for number, j0, width, group in ((0, 0, BANK, BANK), (1, 512, 256, P), (2, 768, P, P), (3, 896, P, P)):
+        for number, j0, width in ((0, 0, BANK), (1, 512, 256), (2, 768, P), (3, 896, P)):
             target = bank(number, "h_bank0_%d" % number)
-            for start in range(0, width, group):
-                for g in range(PASSES):
-                    first_product(target[:, start : start + group], g, 0, j0 + start, group)
-            copy = nc.vector.tensor_copy if number == 1 else nc.scalar.copy
-            copy(h[0][:, j0 : j0 + width], target[:, 0:width])
-        quantize_low(1, 1, behind=19712)
-        quantize_high(1, (2, 3), copy_behind="w1_scale10", apart=True)
-        for t in range(1, PACK):
+            for g in range(PASSES):
+                first_product(target[:, 0:width], g, 0, j0, width)
+            nc.scalar.copy(h[0][:, j0 : j0 + width], target[:, 0:width])
+
+        def make_h(t):
             targets = [bank(H_BANKS[t] + half, "h_bank%d%d" % (t, half)) for half in range(2)]
             for g in range(PASSES):
                 for half in range(2):
                     first_product(targets[half][:], g, t, BANK * half, BANK)
+            return targets
+
+        def empty_h(t, targets):
             for half in range(2):
                 nc.scalar.copy(h[t][:, BANK * half : BANK * (half + 1)], targets[half][:])
 
-        w2_grouped = sb([P, N * PACK], BF16, "w2_grouped", tag="x_code11")
-        nc.scalar.copy(
-            out=w2_grouped[:].rearrange("p (c i t) -> p c t i", i=4, t=PACK),
-            in_=w2_raw[:].rearrange("p t (c i) -> p c t i", i=4),
-        )
-        w2_code = sb([P, N], U32, "w2_code")
-        w2_scale = sb([P, N], U8, "w2_scale")
-        nc.vector.quantize_mx(out=w2_code[:].bitcast(FP8X4), scales=w2_scale[:], in_=w2_grouped[:])
-
         turned = {}
-        for b in range(BLOCKS):
-            turned[b, 0] = turned[b, 1] = bank(TURNED_BANKS[b], "turned%d" % b)
-        rows = [sb([P, H], BF16, "rows%d" % b, tag=28672 if b == 1 else "") for b in range(BLOCKS)]
+        rows = {}
 
-        def gather_terms(tiles, v0, width, behind="", tags=("", ""), bufs=1, order=(0, 1)):
-            name = "%d_%d" % (tiles[0], v0)
+        def products(t, v0, width, places=("", "")):
             columns = slice(v0 // LIST_ROWS, (v0 + width) // LIST_ROWS)
-            products = [
-                sb([P, len(tiles), width], F32, "products%d_%s" % (d, name), tag=tags[d], bufs=bufs) for d in range(2)
-            ]
-            first = sb([P, len(tiles), width], F32, "first" + name, tag=behind)
-            steps = [(n, t, d) for n, t in enumerate(tiles) for d in range(2)]
-            if order != (0, 1):
-                steps = [(n, t, d) for d in order for n, t in enumerate(tiles)]
-            for n, t, d in steps:
-                if True:
-                    nc.vector.tensor_tensor(
-                        products[d][:, n, :],
-                        h[t][:].indirect(neighbour_lists[d][:, columns]),
-                        neg_gate[d][:, v0 : v0 + width],
-                        MULT,
+            made = []
+            for d in range(2):
+                made.append(sb([P, width], F32, "product%d_%d_%d" % (d, t, v0), tag=places[d]))
+                nc.vector.tensor_tensor(
+                    made[d][:], h[t][:].indirect(neighbour_lists[d][:, columns]), neg_gate[d][:, v0 : v0 + width], MULT
+                )
+            return made
+
+        def centres(t, v0, width, place=""):
+            columns = slice(v0 // LIST_ROWS, (v0 + width) // LIST_ROWS)
+            made = sb([P, width], F32, "centre%d_%d" % (t, v0), tag=place)
+            nc.scalar.activation(made[:], h[t][:].indirect(cen_sb[:, columns]), COPY)
+            return [made]
+
+        def add_turned(t, v0, width, terms):
+            u, e = divmod(t, 2)
+            for b in range(v0 // P, (v0 + width) // P):
+                part, place = (e, P * b) if u == 0 else (b // 2, 2 * P * (b % 2) + P * e)
+                if (u, part) not in turned:
+                    turned[u, part] = bank(TURNED_BANKS[u][part], "turned%d%d" % (u, part))
+                for n, term in enumerate(terms):
+                    nc.tensor.matmul(
+                        turned[u, part][:, place : place + P],
+                        lhsT=term[:, P * b - v0 : P * (b + 1) - v0],
+                        rhs=ident[:],
+                        is_transpose=True,
+                        start=(n == 0),
+                        stop=(n == len(terms) - 1),
                     )
-            for n, t in enumerate(tiles):
-                nc.vector.tensor_tensor(first[:, n, :], h[t][:].indirect(cen_sb[:, columns]), products[0][:, n, :], ADD)
-            return first, products[1]
 
-        def add_turned(tiles, v0, width, behind="", tags=("", ""), bufs=1):
-            first, second = gather_terms(tiles, v0, width, behind, tags, bufs)
-            for n, t in enumerate(tiles):
-                for b in range(v0 // P, (v0 + width) // P):
-                    cols = slice(P * b - v0, P * (b + 1) - v0)
-                    for term, start in ((second, True), (first, False)):
-                        nc.tensor.matmul(
-                            turned[b, t // 2][:, P * t : P * (t + 1)],
-                            lhsT=term[:, n, cols],
-                            rhs=ident[:],
-                            is_transpose=True,
-                            start=start,
-                            stop=not start,
-                        )
+        rows_low = sb([P, BLOCKS * 2 * P], BF16, "rows_low")
+        for b in range(BLOCKS):
+            rows[0, b] = rows_low[:, 2 * P * b : 2 * P * (b + 1)]
 
-        def round_pair(b, u):
-            cols = slice(2 * P * u, 2 * P * (u + 1))
-            run = BLOCK_ROWS if u == 0 else P
+        def round_low_rows(s):
             nc.scalar.copy(
-                out=rows[b][:, cols].rearrange("v (q r e) -> v q r e", r=run, e=2),
-                in_=turned[b, u][:, cols].rearrange("v (q e r) -> v q r e", r=run, e=2),
+                out=rows_low[:].rearrange("v (b s q r e) -> v s b q r e", s=2, q=8, r=BLOCK_ROWS, e=2)[:, s],
+                in_=turned[0, s][:].rearrange("v (b q e r) -> v b q r e", q=8, r=BLOCK_ROWS, e=2),
             )
 
-        def turn_back(back, place, b, u):
-            nc.tensor.transpose(
-                back[:, P * place : P * (place + 1)], rows[b][:].bitcast(F32)[:, P * u : P * (u + 1)], ident[:]
+        def round_high_rows(pair, blocks):
+            made = sb([P, blocks * 2 * P], BF16, "rows_high%d" % pair)
+            nc.scalar.copy(
+                out=made[:].rearrange("v (b p e) -> v b p e", p=P, e=2),
+                in_=turned[1, pair][:, 0 : blocks * 2 * P].rearrange("v (b e p) -> v b p e", p=P, e=2),
             )
+            for b in range(blocks):
+                rows[1, 2 * pair + b] = made[:, 2 * P * b : 2 * P * (b + 1)]
+
+        def turn_back(back, place, u, b):
+            nc.tensor.transpose(back[:, P * place : P * (place + 1)], rows[u, b].bitcast(F32), ident[:])
+
+        def interleave(back, b0, blocks):
+            z_grouped = sb([P, blocks * P * PACK], BF16, "z_grouped%d" % b0)
+            nc.scalar.copy(
+                out=z_grouped[:].bitcast(F32).rearrange("p (b v u) -> p b v u", v=P, u=2),
+                in_=back[:, 0 : blocks * 2 * P].rearrange("p (b u v) -> p b v u", v=P, u=2),
+            )
+            return z_grouped
 
         def project(piece, z_grouped, v0, width, behind=""):
             z_code = sb([P, width], U32, "z_code%d" % piece, tag=behind)
             z_scale = sb([P, width], U8, "z_scale%d" % piece)
-            for n, block in enumerate(z_grouped):
-                cols = slice(P * n, P * (n + 1))
-                nc.vector.quantize_mx(out=z_code[:, cols].bitcast(FP8X4), scales=z_scale[:, cols], in_=block[:])
+            nc.vector.quantize_mx(out=z_code[:].bitcast(FP8X4), scales=z_scale[:], in_=z_grouped[:])
             out_bank = bank(OUT_BANKS[piece], "out_bank%d" % piece)
             for a in range(N // P):
                 nc.tensor.matmul_mx(
@@ -290,47 +295,64 @@ def tile_picked_lapl_none_p_kernel(
                     stop=True,
                 )
             result = sb([P, N // P * width], F32, "result%d" % piece)
-            if piece == len(OUT_BANKS) - 1:
-                nc.vector.tensor_copy(result[:], out_bank[:, 0 : N // P * width])
-            else:
-                nc.scalar.copy(result[:], out_bank[:, 0 : N // P * width])
+            copy = nc.vector.tensor_copy if piece == len(OUT_BANKS) - 1 else nc.scalar.copy
+            copy(result[:], out_bank[:, 0 : N // P * width])
             nc.sync.dma_start(
                 out=out.rearrange("(a p) v -> p a v", p=P)[:, :, v0 : v0 + width],
                 in_=result[:].rearrange("p (a v) -> p a v", a=N // P),
             )
 
-        def finish_turned(b):
-            back = bank(BACK_BANKS[b], "back%d" % b)
-            round_pair(b, 1)
-            for u in range(2):
-                turn_back(back, u, b, u)
-            z_grouped = sb([P, P * PACK], BF16, "z_grouped%d" % b)
-            nc.scalar.copy(
-                out=z_grouped[:].bitcast(F32).rearrange("p (v u) -> p v u", u=2),
-                in_=back[:, 0 : 2 * P].rearrange("p (u v) -> p v u", u=2),
-            )
-            return z_grouped
+        terms_0 = products(0, 0, V) + centres(0, 0, V)
+        empty_h(1, make_h(1))
+        empty_h(2, make_h(2))
+        banks_3 = make_h(3)
+        add_turned(0, 0, V, terms_0)
+        terms_1 = products(1, 0, V, (0, 2048)) + centres(1, 0, V, 4096)
+        empty_h(3, banks_3)
+        add_turned(1, 0, V, terms_1)
+        for t in (2, 3):
+            add_turned(t, 0, 2 * P, products(t, 0, 2 * P) + centres(t, 0, 2 * P))
+        add_turned(2, 2 * P, P, products(2, 2 * P, P, (0, 512)) + centres(2, 2 * P, P))
+        add_turned(3, 2 * P, P, products(3, 2 * P, P) + centres(3, 2 * P, P))
+        for s in range(2):
+            round_low_rows(s)
+        round_high_rows(0, 2)
+        round_high_rows(1, 1)
 
-        add_turned((0,), 0, V, behind=17728, tags=("", 19776), bufs=1)
-        add_turned((1,), 0, V)
-        for b in range(BLOCKS):
-            round_pair(b, 0)
+        w2_grouped = sb([P, N * PACK], BF16, "w2_grouped", tag=4096)
+        nc.vector.tensor_copy(
+            out=w2_grouped[:].rearrange("p (c i t) -> p c t i", i=4, t=PACK),
+            in_=w2_raw[:].rearrange("p t (c i) -> p c t i", i=4),
+        )
+        w2_code = sb([P, N], U32, "w2_code")
+        w2_scale = sb([P, N], U8, "w2_scale")
+        nc.vector.quantize_mx(out=w2_code[:].bitcast(FP8X4), scales=w2_scale[:], in_=w2_grouped[:])
+
         last = BLOCKS - 1
-        back_last = bank(BACK_BANKS[2], "back_last")
-        turn_back(back_last, 0, last, 0)
+        back = [bank(number, "back%d" % number) for number in BACK_BANKS]
+        turn_back(back[2], 0, 0, last)
+        for b in range(last):
+            for u in range(2):
+                turn_back(back[b // 2], 2 * (b % 2) + u, u, b)
+        z_0 = interleave(back[0], 0, 2)
         z_last = sb([P, P * PACK], BF16, "z_last")
         nc.scalar.copy(
-            out=z_last[:].bitcast(F32).rearrange("p (v u) -> p v u", u=2)[:, :, 0], in_=back_last[:, 0:P]
+            out=z_last[:].bitcast(F32).rearrange("p (v u) -> p v u", u=2)[:, :, 0], in_=back[2][:, 0:P]
         )
+        z_1 = interleave(back[1], 2, 1)
 
-        add_turned((2,), 0, 2 * P)
-        add_turned((3,), 0, 2 * P)
-        z_0 = [finish_turned(0), finish_turned(1)]
-        turned[2, 1] = bank(TURNED_BANKS[1], "turned_late")
-        add_turned((2, 3), 2 * P, P, tags=(24576, 25600))
-        z_1 = [finish_turned(2)]
         project(0, z_0, 0, 2 * P)
-        first, second = gather_terms((2, 3), P * last, P, tags=(28160, 26624), order=(1, 0))
+        columns = slice(P * last // LIST_ROWS, V // LIST_ROWS)
+        second = sb([P, 2, P], F32, "second", tag=2048)
+        scaled = sb([P, 2, P], F32, "scaled", tag=3072)
+        first = sb([P, 2, P], F32, "first", tag="z_grouped0")
+        for d, made in ((1, second), (0, scaled)):
+            for e in range(2):
+                nc.vector.tensor_tensor(
+                    made[:, e, :], h[2 + e][:].indirect(neighbour_lists[d][:, columns]), neg_gate[d][:, P * last : V], MULT
+                )
+        for e in range(2):
+            nc.vector.tensor_tensor(first[:, e, :], h[2 + e][:].indirect(cen_sb[:, columns]), scaled[:, e, :], ADD)
         nc.vector.tensor_tensor(
             z_last[:].rearrange("p (v u e) -> p v u e", u=2, e=2)[:, :, 1, :],
             first[:].rearrange("p e v -> p v e"),
@@ -338,4 +360,4 @@ def tile_picked_lapl_none_p_kernel(
             ADD,
         )
         project(1, z_1, 2 * P, P)
-        project(2, [z_last], P * last, P, behind="z_grouped2")
+        project(2, z_last, P * last, P, behind="z_grouped2")

@@ -27,7 +27,7 @@ BLOCK_ROWS = 8
 LIST_ROWS = 16
 BLOCKS = V // P
 
-GATE_BANKS = (4, 5)
+GATE_BANKS = (5, 6)
 H_BANKS = (0, 0, 2, 0)
 TURNED_BANKS = ((4, 5), (6, 7))
 BACK_BANKS = (0, 1, 2)
@@ -51,16 +51,16 @@ def tile_picked_lapl_none_p_kernel(
                 return shared.tile(shape, dtype, name=name, align_bytes=64, offset=tag)
             return keep.tile(shape, dtype, name=name, tag=tag or name, align_bytes=64)
 
-        scale_table = sb([P, T], U8, "scale_table")
-        nc.gpsimd.memset(scale_table[:, 0 : T // 2].bitcast(I32), 0)
-        nc.vector.memset(scale_table[:, T // 2 : T].bitcast(I32), 0)
+        scale_table = sb([P, T], U8, "scale_table", tag=15360)
+        nc.gpsimd.memset(scale_table[32:64, :].bitcast(I32), 0)
+        nc.vector.memset(scale_table[64:128, :].bitcast(I32), 0)
 
         def load_list(name, src):
             tile = keep.tile([P, src.shape[1]], U16, name=name)
             nc.sync.dma_start(tile[:], src)
             return tile
 
-        word_table = [sb([P, T], U16, "word_table%d" % g) for g in range(PASSES)]
+        word_table = [sb([P, T], U16, "word_table0", tag=8192), sb([P, T], U16, "word_table1")]
         w1_raw = {}
 
         def load_words(g):
@@ -75,55 +75,49 @@ def tile_picked_lapl_none_p_kernel(
                 w1_raw[g, s] = raw[:, :, H // 2 * n : H // 2 * (n + 1)]
 
         offs_sb = load_list("offs_sb", offs)
+        nc.sync.dma_start(
+            out=scale_table[0:32, :].bitcast(I32), in_=x_scales.bitcast(I32).rearrange("g r c -> r g c")
+        )
         load_words(0)
-        nc.sync.dma_start(out=scale_table[4:20, :].bitcast(I32), in_=x_scales[1].bitcast(I32))
-        for q in range(QUADRANTS):
-            nc.sync.dma_start(
-                out=scale_table[32 * q : 32 * q + 4, :].bitcast(I32),
-                in_=x_scales[0, 4 * q : 4 * q + 4, :].bitcast(I32),
-            )
         gate_cols = sb([P, 2, BLOCKS], F32, "gate_cols")
         nc.sync.dma_start(out=gate_cols[:], in_=gate[:, 0, :].rearrange("d (p b) -> p d b", b=BLOCKS))
         load_w1(0, (0,))
         load_w1(1, (0,))
-        neighbour_lists = [load_list("pos1_sb", pos1), load_list("pos2_sb", pos2)]
-        cen_sb = load_list("cen_sb", cen)
+        neighbour_lists = [load_list("pos1_sb", pos1)]
         load_words(1)
-        load_w1(0, (1,))
+        neighbour_lists.append(load_list("pos2_sb", pos2))
+        cen_sb = load_list("cen_sb", cen)
 
         ident = sb([P, P], F32, "ident")
         make_identity(nc, ident[:])
-        neg_cols = sb([P, 2 * BLOCKS], F32, "neg_cols")
-        nc.scalar.activation(neg_cols[:], gate_cols[:].rearrange("p d b -> p (d b)"), COPY, scale=-1.0)
 
-        scales_0 = sb([P, S], U8, "scales_0")
-        nc.vector.tensor_copy(scales_0[:], scale_table[:].indirect(offs_sb[:]))
-        scales_1 = sb([P, S], U8, "scales_1")
-        nc.vector.memset(scales_1[:].bitcast(I32), 0)
+        picked_scales = sb([P, S], U8, "picked_scales")
+        nc.vector.tensor_copy(picked_scales[:], scale_table[:].indirect(offs_sb[:]))
+        planes = sb([P, PASSES * S], U8, "planes")
+        nc.vector.memset(planes[:].bitcast(I32), 0)
         for q in range(QUADRANTS):
             nc.sync.dma_start(
-                out=scales_1[32 * q : 32 * q + 4, :].bitcast(I32),
-                in_=scales_0[4 * q + 4 : 4 * q + 8, :].bitcast(I32),
+                out=planes[32 * q : 32 * q + 4, :].bitcast(I32).rearrange("p (g c) -> p g c", g=PASSES),
+                in_=picked_scales[8 * q : 8 * q + 8, :].bitcast(I32),
             )
-        x_scale = [scales_0, scales_1]
-        load_w1(1, (1,), behind="scale_table")
-        w2_raw = sb([P, PACK, N], F32, "w2_raw", tag="word_table0")
+        x_scale = [planes[:, S * g : S * (g + 1)] for g in range(PASSES)]
+        load_w1(0, (1,), behind=12288)
+        load_w1(1, (1,), behind=16384)
+        w2_raw = sb([P, PACK, N], F32, "w2_raw", tag="w1_raw10")
         for t in range(PACK):
             nc.sync.dma_start(
                 out=w2_raw[:, t, :], in_=w2.rearrange("(q t r) n -> t q r n", t=PACK, r=BLOCK_ROWS)[t]
             )
 
-        x_code = {}
+        x_code = [sb([P, 2 * S], U8, "x_code%d" % g) for g in range(PASSES)]
         w1_code = {}
         w1_scale = {}
 
-        def gather_words(g, half, first, width, behind=""):
-            if first == 0:
-                x_code[g, half] = sb([P, BANK], U16, "x_code%d%d" % (g, half), tag=behind)
+        def gather_words(g, half, first, width):
             start = half * BANK + first
             columns = slice(start // LIST_ROWS, (start + width) // LIST_ROWS)
             nc.vector.tensor_copy(
-                x_code[g, half][:, first : first + width], word_table[g][:].indirect(offs_sb[:, columns])
+                x_code[g][:, 2 * start : 2 * (start + width)].bitcast(U16), word_table[g][:].indirect(offs_sb[:, columns])
             )
 
         def round_low(g, s, grouped, copy):
@@ -132,10 +126,10 @@ def tile_picked_lapl_none_p_kernel(
                 in_=w1_raw[g, s].rearrange("p j (q c i) -> p q c j i", c=8, i=4)[:, :, 0:4],
             )
 
-        def round_high(g, s, grouped, copy):
+        def round_high(g, s, grouped, copy, tiles=(0, 1)):
             view = grouped.rearrange("p (e s q c i j) -> p e s q c j i", e=2, s=2, c=2, i=4, j=PACK)
             dealt = w1_raw[g, s].rearrange("p j (q t c i) -> p t q c j i", t=PACK, c=2, i=4)
-            for e in range(2):
+            for e in tiles:
                 copy(out=view[:, e, s], in_=dealt[:, 2 + e])
 
         def quantize_w1(g, tiles, grouped, behind=""):
@@ -146,61 +140,63 @@ def tile_picked_lapl_none_p_kernel(
                 w1_code[g, t] = code[:, P * e : P * (e + 1)]
                 w1_scale[g, t] = scale[:, P * e : P * (e + 1)]
 
-        neg_gate = []
-        for d in range(2):
-            spread = bank(GATE_BANKS[d], "spread%d" % d)
-            for b in range(BLOCKS):
-                col = BLOCKS * d + b
-                nc.tensor.transpose(
-                    spread[:, P * b : P * (b + 1)], neg_cols[:, col : col + 1].to_broadcast([P, P]), ident[:]
-                )
-            neg_gate.append(sb([P, V], F32, "neg_gate%d" % d))
-            nc.scalar.copy(
-                out=neg_gate[d][:].rearrange("p (n b) -> p n b", b=BLOCKS),
-                in_=spread[:].rearrange("p (b n) -> p n b", b=BLOCKS),
-            )
-
         wide = P * PACK
         grouped = {
             (g, t): sb([P, n * wide], BF16, "w1_grouped%d%d" % (g, t))
             for g, t, n in ((0, 0, 1), (1, 0, 1), (0, 1, 3), (1, 1, 1), (1, 2, 2))
         }
         gather_words(0, 0, 0, BANK)
-        gather_words(0, 1, 0, BANK, behind="gate_cols")
+        gather_words(0, 1, 0, BANK)
         for g in range(PASSES):
             round_low(g, 0, grouped[g, 0][:], nc.scalar.copy)
             quantize_w1(g, (0,), grouped[g, 0][:])
         round_high(0, 0, grouped[0, 1][:, wide : 3 * wide], nc.scalar.copy)
         round_high(1, 0, grouped[1, 2][:], nc.scalar.copy)
-        round_low(0, 1, grouped[0, 1][:, 0:wide], nc.scalar.copy)
-        round_high(0, 1, grouped[0, 1][:, wide : 3 * wide], nc.scalar.copy)
-        gather_words(1, 0, 0, BANK)
-        gather_words(1, 1, 0, BANK // 2)
-        gather_words(1, 1, BANK // 2, BANK // 2)
-        quantize_w1(0, (1, 2, 3), grouped[0, 1][:], behind="word_table1")
+        neg_gate = []
+        for d in range(2):
+            spread = bank(GATE_BANKS[d], "spread%d" % d)
+            for b in range(BLOCKS):
+                nc.tensor.transpose(
+                    spread[:, P * b : P * (b + 1)], gate_cols[:, d, b : b + 1].to_broadcast([P, P]), ident[:]
+                )
+            neg_gate.append(sb([P, V], F32, "neg_gate%d" % d))
+            nc.scalar.activation(
+                neg_gate[d][:].rearrange("p (n b) -> p n b", b=BLOCKS),
+                spread[:].rearrange("p (b n) -> p n b", b=BLOCKS),
+                COPY,
+                scale=-1.0,
+            )
+        for half in range(2):
+            for first in (0, BANK // 2):
+                gather_words(1, half, first, BANK // 2)
+        round_low(0, 1, grouped[0, 1][:, 0:wide], nc.vector.tensor_copy)
+        round_high(0, 1, grouped[0, 1][:, wide : 3 * wide], nc.vector.tensor_copy)
+        quantize_w1(0, (1, 2, 3), grouped[0, 1][:])
         round_low(1, 1, grouped[1, 1][:], nc.vector.tensor_copy)
-        round_high(1, 1, grouped[1, 2][:], nc.vector.tensor_copy)
+        round_high(1, 1, grouped[1, 2][:], nc.vector.tensor_copy, (0,))
         quantize_w1(1, (1,), grouped[1, 1][:])
+        round_high(1, 1, grouped[1, 2][:], nc.vector.tensor_copy, (1,))
         quantize_w1(1, (2, 3), grouped[1, 2][:])
 
         h = [sb([P, S], F32, "h%d" % t) for t in range(PACK)]
 
         def first_product(target, g, t, j0, width):
-            half, start = divmod(j0, BANK)
             nc.tensor.matmul_mx(
                 out=target,
                 lhsT=w1_code[g, t].bitcast(FP8X4),
                 lhsT_scale=w1_scale[g, t],
-                rhs=x_code[g, half][:, start : start + width].bitcast(FP4X4),
+                rhs=x_code[g][:, 2 * j0 : 2 * (j0 + width)].bitcast(FP4X4),
                 rhs_scale=x_scale[g][:, j0 : j0 + width],
                 start=(g == 0),
                 stop=(g == PASSES - 1),
             )
 
-        for number, j0, width in ((0, 0, BANK), (1, 512, 256), (2, 768, P), (3, 896, P)):
-            target = bank(number, "h_bank0_%d" % number)
-            for g in range(PASSES):
+        pieces = ((4, 0, 256), (0, 256, 256), (1, 512, 256), (2, 768, P), (3, 896, P))
+        targets = [bank(number, "h_bank0_%d" % number) for number, j0, width in pieces]
+        for g in range(PASSES):
+            for target, (number, j0, width) in zip(targets, pieces):
                 first_product(target[:, 0:width], g, 0, j0, width)
+        for target, (number, j0, width) in zip(targets, pieces):
             nc.scalar.copy(h[0][:, j0 : j0 + width], target[:, 0:width])
 
         def make_h(t):
@@ -302,7 +298,7 @@ def tile_picked_lapl_none_p_kernel(
                 in_=result[:].rearrange("p (a v) -> p a v", a=N // P),
             )
 
-        terms_0 = products(0, 0, V) + centres(0, 0, V)
+        terms_0 = products(0, 0, V, ("w1_grouped11", "w1_grouped12")) + centres(0, 0, V)
         empty_h(1, make_h(1))
         empty_h(2, make_h(2))
         banks_3 = make_h(3)
@@ -312,12 +308,11 @@ def tile_picked_lapl_none_p_kernel(
         add_turned(1, 0, V, terms_1)
         for t in (2, 3):
             add_turned(t, 0, 2 * P, products(t, 0, 2 * P) + centres(t, 0, 2 * P))
-        add_turned(2, 2 * P, P, products(2, 2 * P, P, (0, 512)) + centres(2, 2 * P, P))
-        add_turned(3, 2 * P, P, products(3, 2 * P, P) + centres(3, 2 * P, P))
         for s in range(2):
             round_low_rows(s)
         round_high_rows(0, 2)
-        round_high_rows(1, 1)
+        terms_2 = products(2, 2 * P, P, (0, 512)) + centres(2, 2 * P, P)
+        terms_3 = products(3, 2 * P, P) + centres(3, 2 * P, P)
 
         w2_grouped = sb([P, N * PACK], BF16, "w2_grouped", tag=4096)
         nc.vector.tensor_copy(
@@ -330,22 +325,28 @@ def tile_picked_lapl_none_p_kernel(
 
         last = BLOCKS - 1
         back = [bank(number, "back%d" % number) for number in BACK_BANKS]
-        turn_back(back[2], 0, 0, last)
-        for b in range(last):
+        for b in range(2):
             for u in range(2):
-                turn_back(back[b // 2], 2 * (b % 2) + u, u, b)
+                turn_back(back[0], 2 * b + u, u, b)
+        add_turned(2, 2 * P, P, terms_2)
+        add_turned(3, 2 * P, P, terms_3)
+        turn_back(back[2], 0, 0, last)
         z_0 = interleave(back[0], 0, 2)
+        round_high_rows(1, 1)
+        for u in range(2):
+            turn_back(back[1], u, u, 2)
+        z_1 = interleave(back[1], 2, 1)
         z_last = sb([P, P * PACK], BF16, "z_last")
         nc.scalar.copy(
             out=z_last[:].bitcast(F32).rearrange("p (v u) -> p v u", u=2)[:, :, 0], in_=back[2][:, 0:P]
         )
-        z_1 = interleave(back[1], 2, 1)
 
         project(0, z_0, 0, 2 * P)
+        project(1, z_1, 2 * P, P)
         columns = slice(P * last // LIST_ROWS, V // LIST_ROWS)
         second = sb([P, 2, P], F32, "second", tag=2048)
         scaled = sb([P, 2, P], F32, "scaled", tag=3072)
-        first = sb([P, 2, P], F32, "first", tag="z_grouped0")
+        first = sb([P, 2, P], F32, "first", tag="rows_high1")
         for d, made in ((1, second), (0, scaled)):
             for e in range(2):
                 nc.vector.tensor_tensor(
@@ -355,9 +356,8 @@ def tile_picked_lapl_none_p_kernel(
             nc.vector.tensor_tensor(first[:, e, :], h[2 + e][:].indirect(cen_sb[:, columns]), scaled[:, e, :], ADD)
         nc.vector.tensor_tensor(
             z_last[:].rearrange("p (v u e) -> p v u e", u=2, e=2)[:, :, 1, :],
-            first[:].rearrange("p e v -> p v e"),
             second[:].rearrange("p e v -> p v e"),
+            first[:].rearrange("p e v -> p v e"),
             ADD,
         )
-        project(1, z_1, 2 * P, P)
-        project(2, z_last, P * last, P, behind="z_grouped2")
+        project(2, z_last, P * last, P)

@@ -28,10 +28,10 @@ LIST_ROWS = 16
 BLOCKS = V // P
 
 GATE_BANKS = (5, 6)
-H_BANKS = (0, 0, 2, 0)
+H_BANKS = (0, 0, 2, 2)
 TURNED_BANKS = ((4, 5), (6, 7))
 BACK_BANKS = (0, 1, 2)
-OUT_BANKS = (3, 4, 5)
+OUT_BANKS = (1, 4, 5)
 
 
 def tile_picked_lapl_none_p_kernel(
@@ -308,11 +308,12 @@ def tile_picked_lapl_none_p_kernel(
         add_turned(1, 0, V, terms_1)
         for t in (2, 3):
             add_turned(t, 0, 2 * P, products(t, 0, 2 * P) + centres(t, 0, 2 * P))
+        add_turned(2, 2 * P, P, products(2, 2 * P, P, (0, 512)) + centres(2, 2 * P, P))
+        add_turned(3, 2 * P, P, products(3, 2 * P, P) + centres(3, 2 * P, P))
         for s in range(2):
             round_low_rows(s)
         round_high_rows(0, 2)
-        terms_2 = products(2, 2 * P, P, (0, 512)) + centres(2, 2 * P, P)
-        terms_3 = products(3, 2 * P, P) + centres(3, 2 * P, P)
+        round_high_rows(1, 1)
 
         w2_grouped = sb([P, N * PACK], BF16, "w2_grouped", tag=4096)
         nc.vector.tensor_copy(
@@ -328,13 +329,10 @@ def tile_picked_lapl_none_p_kernel(
         for b in range(2):
             for u in range(2):
                 turn_back(back[0], 2 * b + u, u, b)
-        add_turned(2, 2 * P, P, terms_2)
-        add_turned(3, 2 * P, P, terms_3)
-        turn_back(back[2], 0, 0, last)
-        z_0 = interleave(back[0], 0, 2)
-        round_high_rows(1, 1)
         for u in range(2):
             turn_back(back[1], u, u, 2)
+        turn_back(back[2], 0, 0, last)
+        z_0 = interleave(back[0], 0, 2)
         z_1 = interleave(back[1], 2, 1)
         z_last = sb([P, P * PACK], BF16, "z_last")
         nc.scalar.copy(
@@ -345,8 +343,8 @@ def tile_picked_lapl_none_p_kernel(
         project(1, z_1, 2 * P, P)
         columns = slice(P * last // LIST_ROWS, V // LIST_ROWS)
         second = sb([P, 2, P], F32, "second", tag=2048)
-        scaled = sb([P, 2, P], F32, "scaled", tag=3072)
-        first = sb([P, 2, P], F32, "first", tag="rows_high1")
+        scaled = sb([P, 2, P], F32, "scaled", tag="rows_high0")
+        first = sb([P, 2, P], F32, "first")
         for d, made in ((1, second), (0, scaled)):
             for e in range(2):
                 nc.vector.tensor_tensor(

@@ -28,10 +28,10 @@ LIST_ROWS = 16
 BLOCKS = V // P
 
 GATE_BANKS = (5, 6)
-H_BANKS = (0, 0, 2, 2)
-TURNED_BANKS = ((4, 5), (6, 7))
-BACK_BANKS = (0, 1, 2)
-OUT_BANKS = (1, 4, 5)
+H_BANKS = (0, 0, 2, 0)
+TURNED_BANKS = ((4, 5), (6,))
+BACK_BANKS = (0, 6)
+OUT_BANKS = (1, 2, 3)
 
 
 def tile_picked_lapl_none_p_kernel(
@@ -278,7 +278,9 @@ def tile_picked_lapl_none_p_kernel(
         def project(piece, z_grouped, v0, width, behind=""):
             z_code = sb([P, width], U32, "z_code%d" % piece, tag=behind)
             z_scale = sb([P, width], U8, "z_scale%d" % piece)
-            nc.vector.quantize_mx(out=z_code[:].bitcast(FP8X4), scales=z_scale[:], in_=z_grouped[:])
+            for n, block in enumerate(z_grouped):
+                cols = slice(P * n, P * (n + 1))
+                nc.vector.quantize_mx(out=z_code[:, cols].bitcast(FP8X4), scales=z_scale[:, cols], in_=block)
             out_bank = bank(OUT_BANKS[piece], "out_bank%d" % piece)
             for a in range(N // P):
                 nc.tensor.matmul_mx(
@@ -308,54 +310,67 @@ def tile_picked_lapl_none_p_kernel(
         add_turned(1, 0, V, terms_1)
         for t in (2, 3):
             add_turned(t, 0, 2 * P, products(t, 0, 2 * P) + centres(t, 0, 2 * P))
-        add_turned(2, 2 * P, P, products(2, 2 * P, P, (0, 512)) + centres(2, 2 * P, P))
-        add_turned(3, 2 * P, P, products(3, 2 * P, P) + centres(3, 2 * P, P))
         for s in range(2):
             round_low_rows(s)
         round_high_rows(0, 2)
-        round_high_rows(1, 1)
+        back = bank(BACK_BANKS[0], "back_whole")
+        for b in range(2):
+            for u in range(2):
+                turn_back(back, 2 * b + u, u, b)
+        z_0 = [interleave(back[:, 2 * P * b : 2 * P * (b + 1)], b, 1) for b in range(2)]
+        back_low = bank(BACK_BANKS[1], "back_low")
+        z_late = sb([P, 2 * P * PACK], BF16, "z_late")
+        for n in range(2):
+            turn_back(back_low, n, 0, 2 + n)
+        nc.scalar.copy(
+            out=z_late[:].bitcast(F32).rearrange("p (v u) -> p v u", u=2)[:, :, 0], in_=back_low[:, 0 : 2 * P]
+        )
 
+        second = sb([P, 2, 2 * P], F32, "second", tag=2048)
+        for e in range(2):
+            nc.vector.tensor_tensor(
+                second[:, e, :],
+                h[2 + e][:].indirect(neighbour_lists[1][:, 2 * P // LIST_ROWS : V // LIST_ROWS]),
+                neg_gate[1][:, 2 * P : V],
+                MULT,
+            )
+
+        def gather_first(b, behind, sums_behind=""):
+            columns = slice(P * b // LIST_ROWS, P * (b + 1) // LIST_ROWS)
+            scaled = sb([P, 2, P], F32, "scaled%d" % b, tag=behind)
+            first = sb([P, 2, P], F32, "first%d" % b, tag=sums_behind)
+            for e in range(2):
+                nc.vector.tensor_tensor(
+                    scaled[:, e, :],
+                    h[2 + e][:].indirect(neighbour_lists[0][:, columns]),
+                    neg_gate[0][:, P * b : P * (b + 1)],
+                    MULT,
+                )
+            for e in range(2):
+                nc.vector.tensor_tensor(first[:, e, :], h[2 + e][:].indirect(cen_sb[:, columns]), scaled[:, e, :], ADD)
+            return first
+
+        def add_late(b, first):
+            cols = slice(P * (b - 2), P * (b - 1))
+            nc.vector.tensor_tensor(
+                z_late[:].rearrange("p (v u e) -> p v u e", u=2, e=2)[:, cols, 1, :],
+                first[:].rearrange("p e v -> p v e"),
+                second[:, :, cols].rearrange("p e v -> p v e"),
+                ADD,
+            )
+
+        first_2 = gather_first(2, 0)
         w2_grouped = sb([P, N * PACK], BF16, "w2_grouped", tag=4096)
         nc.vector.tensor_copy(
             out=w2_grouped[:].rearrange("p (c i t) -> p c t i", i=4, t=PACK),
             in_=w2_raw[:].rearrange("p t (c i) -> p c t i", i=4),
         )
+        add_late(2, first_2)
         w2_code = sb([P, N], U32, "w2_code")
         w2_scale = sb([P, N], U8, "w2_scale")
         nc.vector.quantize_mx(out=w2_code[:].bitcast(FP8X4), scales=w2_scale[:], in_=w2_grouped[:])
-
-        last = BLOCKS - 1
-        back = [bank(number, "back%d" % number) for number in BACK_BANKS]
-        for b in range(2):
-            for u in range(2):
-                turn_back(back[0], 2 * b + u, u, b)
-        for u in range(2):
-            turn_back(back[1], u, u, 2)
-        turn_back(back[2], 0, 0, last)
-        z_0 = interleave(back[0], 0, 2)
-        z_1 = interleave(back[1], 2, 1)
-        z_last = sb([P, P * PACK], BF16, "z_last")
-        nc.scalar.copy(
-            out=z_last[:].bitcast(F32).rearrange("p (v u) -> p v u", u=2)[:, :, 0], in_=back[2][:, 0:P]
-        )
-
-        project(0, z_0, 0, 2 * P)
-        project(1, z_1, 2 * P, P)
-        columns = slice(P * last // LIST_ROWS, V // LIST_ROWS)
-        second = sb([P, 2, P], F32, "second", tag=2048)
-        scaled = sb([P, 2, P], F32, "scaled", tag="rows_high0")
-        first = sb([P, 2, P], F32, "first")
-        for d, made in ((1, second), (0, scaled)):
-            for e in range(2):
-                nc.vector.tensor_tensor(
-                    made[:, e, :], h[2 + e][:].indirect(neighbour_lists[d][:, columns]), neg_gate[d][:, P * last : V], MULT
-                )
-        for e in range(2):
-            nc.vector.tensor_tensor(first[:, e, :], h[2 + e][:].indirect(cen_sb[:, columns]), scaled[:, e, :], ADD)
-        nc.vector.tensor_tensor(
-            z_last[:].rearrange("p (v u e) -> p v u e", u=2, e=2)[:, :, 1, :],
-            second[:].rearrange("p e v -> p v e"),
-            first[:].rearrange("p e v -> p v e"),
-            ADD,
-        )
-        project(2, z_last, P * last, P)
+        project(0, [block[:] for block in z_0], 0, 2 * P)
+        first = gather_first(3, 1024, "z_grouped0")
+        project(1, [z_late[:, 0 : P * PACK]], 2 * P, P)
+        add_late(3, first)
+        project(2, [z_late[:, P * PACK : 2 * P * PACK]], 3 * P, P)

@@ -312,10 +312,15 @@ def tile_picked_lapl_none_p_kernel(
             add_turned(t, 0, 2 * P, products(t, 0, 2 * P) + centres(t, 0, 2 * P))
         for s in range(2):
             round_low_rows(s)
+        w2_grouped = sb([P, N * PACK], BF16, "w2_grouped", tag=4096)
+        nc.scalar.copy(
+            out=w2_grouped[:].rearrange("p (c i t) -> p c t i", i=4, t=PACK),
+            in_=w2_raw[:].rearrange("p t (c i) -> p c t i", i=4),
+        )
         round_high_rows(0, 2)
         back = bank(BACK_BANKS[0], "back_whole")
-        for b in range(2):
-            for u in range(2):
+        for u in range(2):
+            for b in range(2):
                 turn_back(back, 2 * b + u, u, b)
         z_0 = [interleave(back[:, 2 * P * b : 2 * P * (b + 1)], b, 1) for b in range(2)]
         back_low = bank(BACK_BANKS[1], "back_low")
@@ -360,11 +365,6 @@ def tile_picked_lapl_none_p_kernel(
             )
 
         first_2 = gather_first(2, 0)
-        w2_grouped = sb([P, N * PACK], BF16, "w2_grouped", tag=4096)
-        nc.vector.tensor_copy(
-            out=w2_grouped[:].rearrange("p (c i t) -> p c t i", i=4, t=PACK),
-            in_=w2_raw[:].rearrange("p t (c i) -> p c t i", i=4),
-        )
         add_late(2, first_2)
         w2_code = sb([P, N], U32, "w2_code")
         w2_scale = sb([P, N], U8, "w2_scale")

@@ -143,14 +143,14 @@ def tile_picked_lapl_none_p_kernel(
         wide = P * PACK
         grouped = {
             (g, t): sb([P, n * wide], BF16, "w1_grouped%d%d" % (g, t))
-            for g, t, n in ((0, 0, 1), (1, 0, 1), (0, 1, 3), (1, 1, 1), (1, 2, 2))
+            for g, t, n in ((0, 0, 1), (1, 0, 1), (0, 1, 1), (0, 2, 2), (1, 1, 1), (1, 2, 2))
         }
         gather_words(0, 0, 0, BANK)
         gather_words(0, 1, 0, BANK)
         for g in range(PASSES):
             round_low(g, 0, grouped[g, 0][:], nc.scalar.copy)
             quantize_w1(g, (0,), grouped[g, 0][:])
-        round_high(0, 0, grouped[0, 1][:, wide : 3 * wide], nc.scalar.copy)
+        round_high(0, 0, grouped[0, 2][:], nc.scalar.copy)
         round_high(1, 0, grouped[1, 2][:], nc.scalar.copy)
         neg_gate = []
         for d in range(2):
@@ -169,13 +169,14 @@ def tile_picked_lapl_none_p_kernel(
         for half in range(2):
             for first in (0, BANK // 2):
                 gather_words(1, half, first, BANK // 2)
-        round_low(0, 1, grouped[0, 1][:, 0:wide], nc.vector.tensor_copy)
-        round_high(0, 1, grouped[0, 1][:, wide : 3 * wide], nc.vector.tensor_copy)
-        quantize_w1(0, (1, 2, 3), grouped[0, 1][:])
+        round_low(0, 1, grouped[0, 1][:], nc.vector.tensor_copy)
+        round_high(0, 1, grouped[0, 2][:], nc.vector.tensor_copy, (0,))
+        quantize_w1(0, (1,), grouped[0, 1][:])
         round_low(1, 1, grouped[1, 1][:], nc.vector.tensor_copy)
-        round_high(1, 1, grouped[1, 2][:], nc.vector.tensor_copy, (0,))
+        round_high(0, 1, grouped[0, 2][:], nc.vector.tensor_copy, (1,))
         quantize_w1(1, (1,), grouped[1, 1][:])
-        round_high(1, 1, grouped[1, 2][:], nc.vector.tensor_copy, (1,))
+        round_high(1, 1, grouped[1, 2][:], nc.vector.tensor_copy)
+        quantize_w1(0, (2, 3), grouped[0, 2][:])
         quantize_w1(1, (2, 3), grouped[1, 2][:])
 
         h = [sb([P, S], F32, "h%d" % t) for t in range(PACK)]
@@ -308,16 +309,16 @@ def tile_picked_lapl_none_p_kernel(
         terms_1 = products(1, 0, V, (0, 2048)) + centres(1, 0, V, 4096)
         empty_h(3, banks_3)
         add_turned(1, 0, V, terms_1)
-        for t in (2, 3):
-            add_turned(t, 0, 2 * P, products(t, 0, 2 * P) + centres(t, 0, 2 * P))
+        add_turned(2, 0, 2 * P, products(2, 0, 2 * P) + centres(2, 0, 2 * P))
+        add_turned(3, 0, 2 * P, products(3, 0, 2 * P) + centres(3, 0, 2 * P, 6144))
         for s in range(2):
             round_low_rows(s)
-        w2_grouped = sb([P, N * PACK], BF16, "w2_grouped", tag=4096)
+        round_high_rows(0, 2)
+        w2_grouped = sb([P, N * PACK], BF16, "w2_grouped", tag=6144)
         nc.scalar.copy(
             out=w2_grouped[:].rearrange("p (c i t) -> p c t i", i=4, t=PACK),
             in_=w2_raw[:].rearrange("p t (c i) -> p c t i", i=4),
         )
-        round_high_rows(0, 2)
         back = bank(BACK_BANKS[0], "back_whole")
         for u in range(2):
             for b in range(2):

@@ -31,7 +31,7 @@ GATE_BANKS = (5, 6)
 H_BANKS = (0, 0, 2, 0)
 TURNED_BANKS = ((4, 5), (6,))
 BACK_BANKS = (0, 6)
-OUT_BANKS = (1, 2, 3)
+OUT_BANKS = (1, 2, 3, 4)
 
 
 def tile_picked_lapl_none_p_kernel(
@@ -276,16 +276,16 @@ def tile_picked_lapl_none_p_kernel(
             )
             return z_grouped
 
-        def project(piece, z_grouped, v0, width, behind=""):
-            z_code = sb([P, width], U32, "z_code%d" % piece, tag=behind)
+        def project(piece, blocks, banks):
+            width = P * len(blocks)
+            z_code = sb([P, width], U32, "z_code%d" % piece)
             z_scale = sb([P, width], U8, "z_scale%d" % piece)
-            for n, block in enumerate(z_grouped):
+            for n, block in enumerate(blocks):
                 cols = slice(P * n, P * (n + 1))
                 nc.vector.quantize_mx(out=z_code[:, cols].bitcast(FP8X4), scales=z_scale[:, cols], in_=block)
-            out_bank = bank(OUT_BANKS[piece], "out_bank%d" % piece)
             for a in range(N // P):
                 nc.tensor.matmul_mx(
-                    out=out_bank[:, width * a : width * (a + 1)],
+                    out=banks[a],
                     lhsT=w2_code[:, P * a : P * (a + 1)].bitcast(FP8X4),
                     lhsT_scale=w2_scale[:, P * a : P * (a + 1)],
                     rhs=z_code[:].bitcast(FP8X4),
@@ -293,13 +293,11 @@ def tile_picked_lapl_none_p_kernel(
                     start=True,
                     stop=True,
                 )
-            result = sb([P, N // P * width], F32, "result%d" % piece)
-            copy = nc.vector.tensor_copy if piece == len(OUT_BANKS) - 1 else nc.scalar.copy
-            copy(result[:], out_bank[:, 0 : N // P * width])
-            nc.sync.dma_start(
-                out=out.rearrange("(a p) v -> p a v", p=P)[:, :, v0 : v0 + width],
-                in_=result[:].rearrange("p (a v) -> p a v", a=N // P),
-            )
+
+        def store(place, target, copy, name, behind=""):
+            result = sb([P, 2 * P], F32, name, tag=behind)
+            copy(result[:], place)
+            nc.sync.dma_start(out=target, in_=result[:].rearrange("p (a v) -> p a v", a=target.shape[1]))
 
         terms_0 = products(0, 0, V, ("w1_grouped11", "w1_grouped12")) + centres(0, 0, V)
         empty_h(1, make_h(1))
@@ -314,11 +312,13 @@ def tile_picked_lapl_none_p_kernel(
         for s in range(2):
             round_low_rows(s)
         round_high_rows(0, 2)
-        w2_grouped = sb([P, N * PACK], BF16, "w2_grouped", tag=6144)
-        nc.scalar.copy(
-            out=w2_grouped[:].rearrange("p (c i t) -> p c t i", i=4, t=PACK),
-            in_=w2_raw[:].rearrange("p t (c i) -> p c t i", i=4),
-        )
+        w2_grouped = []
+        for a, place in enumerate((4096, 6144)):
+            w2_grouped.append(sb([P, P * PACK], BF16, "w2_grouped%d" % a, tag=place))
+            nc.scalar.copy(
+                out=w2_grouped[a][:].rearrange("p (c i t) -> p c t i", i=4, t=PACK),
+                in_=w2_raw[:, :, P * a : P * (a + 1)].rearrange("p t (c i) -> p c t i", i=4),
+            )
         back = bank(BACK_BANKS[0], "back_whole")
         for u in range(2):
             for b in range(2):
@@ -328,6 +328,11 @@ def tile_picked_lapl_none_p_kernel(
         z_late = sb([P, 2 * P * PACK], BF16, "z_late")
         for n in range(2):
             turn_back(back_low, n, 0, 2 + n)
+        first = sb([P, 2, P], F32, "centre_last", tag="rows_low")
+        for e in range(2):
+            nc.scalar.activation(
+                first[:, e, :], h[2 + e][:].indirect(cen_sb[:, 3 * P // LIST_ROWS : V // LIST_ROWS]), COPY
+            )
         nc.scalar.copy(
             out=z_late[:].bitcast(F32).rearrange("p (v u) -> p v u", u=2)[:, :, 0], in_=back_low[:, 0 : 2 * P]
         )
@@ -356,22 +361,37 @@ def tile_picked_lapl_none_p_kernel(
                 nc.vector.tensor_tensor(first[:, e, :], h[2 + e][:].indirect(cen_sb[:, columns]), scaled[:, e, :], ADD)
             return first
 
-        def add_late(b, first):
+        def add_late(b, first, other):
             cols = slice(P * (b - 2), P * (b - 1))
             nc.vector.tensor_tensor(
                 z_late[:].rearrange("p (v u e) -> p v u e", u=2, e=2)[:, cols, 1, :],
                 first[:].rearrange("p e v -> p v e"),
-                second[:, :, cols].rearrange("p e v -> p v e"),
+                other.rearrange("p e v -> p v e"),
                 ADD,
             )
 
         first_2 = gather_first(2, 0)
-        add_late(2, first_2)
+        add_late(2, first_2, second[:, :, 0:P])
         w2_code = sb([P, N], U32, "w2_code")
         w2_scale = sb([P, N], U8, "w2_scale")
-        nc.vector.quantize_mx(out=w2_code[:].bitcast(FP8X4), scales=w2_scale[:], in_=w2_grouped[:])
-        project(0, [block[:] for block in z_0], 0, 2 * P)
-        first = gather_first(3, 1024, "z_grouped0")
-        project(1, [z_late[:, 0 : P * PACK]], 2 * P, P)
-        add_late(3, first)
-        project(2, [z_late[:, P * PACK : 2 * P * PACK]], 3 * P, P)
+        for a in range(N // P):
+            cols = slice(P * a, P * (a + 1))
+            nc.vector.quantize_mx(out=w2_code[:, cols].bitcast(FP8X4), scales=w2_scale[:, cols], in_=w2_grouped[a][:])
+        out_banks = [bank(number, "out_bank%d" % number) for number in OUT_BANKS]
+        rows_out = out.rearrange("(a p) v -> p a v", p=P)
+        project(0, [block[:] for block in z_0], [out_banks[a][:, 0 : 2 * P] for a in range(2)])
+        store(out_banks[0][:, 0 : 2 * P], rows_out[:, 0:1, 0 : 2 * P], nc.scalar.copy, "result0")
+        columns = slice(3 * P // LIST_ROWS, V // LIST_ROWS)
+        scaled = sb([P, 2, P], F32, "scaled3", tag=1024)
+        both = sb([P, 2, P], F32, "both")
+        for e in range(2):
+            nc.vector.tensor_tensor(
+                scaled[:, e, :], h[2 + e][:].indirect(neighbour_lists[0][:, columns]), neg_gate[0][:, 3 * P : V], MULT
+            )
+        nc.vector.tensor_tensor(both[:], scaled[:], second[:, :, P : 2 * P], ADD)
+        add_late(3, first, both[:])
+        project(1, [z_late[:, 0 : P * PACK]], [out_banks[2][:, P * a : P * (a + 1)] for a in range(2)])
+        store(out_banks[2][:, 0 : 2 * P], rows_out[:, :, 2 * P : 3 * P], nc.scalar.copy, "result2")
+        project(2, [z_late[:, P * PACK : 2 * P * PACK]], [out_banks[3][:, P * a : P * (a + 1)] for a in range(2)])
+        store(out_banks[1][:, 0 : 2 * P], rows_out[:, 1:2, 0 : 2 * P], nc.vector.tensor_copy, "result1", "both")
+        store(out_banks[3][:, 0 : 2 * P], rows_out[:, :, 3 * P : V], nc.vector.tensor_copy, "result3")

from contextlib import ExitStack

import concourse.mybir as mybir
from concourse.masks import make_identity

K, T, S, V, H, N = 1024, 2048, 1024, 512, 512, 256
FLOPS = 2 * K * H * S + 2 * H * N * V

F32 = mybir.dt.float32
BF16 = mybir.dt.bfloat16
I32 = mybir.dt.int32
U32 = mybir.dt.uint32
U16 = mybir.dt.uint16
U8 = mybir.dt.uint8
FP8X4 = mybir.dt.float8_e4m3fn_x4
FP4X4 = mybir.dt.float4_e2m1fn_x4
COPY = mybir.ActivationFunctionType.Copy
ADD = mybir.AluOpType.add
MULT = mybir.AluOpType.mult

P = 128
PACK = 4
BANK = 512
PASSES = K // (P * PACK)
QUADRANTS = 4
BLOCK_ROWS = 8
LIST_ROWS = 16
BLOCKS = V // P

GATE_BANKS = (5, 6)
H_BANKS = (0, 0, 2, 0)
TURNED_BANKS = ((4, 5), (6,))
BACK_BANKS = (0, 6)
OUT_BANKS = (1, 2, 3, 4)


def tile_picked_lapl_none_p_kernel(
    tc, x_words, x_scales, w1, w2, gate, offs, cen, pos1, pos2, out
):
    nc = tc.nc
    with ExitStack() as ctx:
        keep = ctx.enter_context(tc.tile_pool(name="keep", bufs=1))
        shared = ctx.enter_context(tc.tile_pool(name="shared", bufs=1))
        psum = ctx.enter_context(tc.psum_pool(name="psum", bufs=1))

        def bank(number, name):
            return psum.tile([P, BANK], F32, name=name, tag="bank%d" % number)

        def sb(shape, dtype, name, tag=""):
            if isinstance(tag, int):
                return shared.tile(shape, dtype, name=name, align_bytes=64, offset=tag)
            return keep.tile(shape, dtype, name=name, tag=tag or name, align_bytes=64)

        scale_table = sb([P, T], U8, "scale_table", tag=15360)
        nc.gpsimd.memset(scale_table[32:64, :].bitcast(I32), 0)
        nc.vector.memset(scale_table[64:128, :].bitcast(I32), 0)

        def load_list(name, src):
            tile = keep.tile([P, src.shape[1]], U16, name=name)
            nc.sync.dma_start(tile[:], src)
            return tile

        word_table = [sb([P, T], U16, "word_table0", tag=8192), sb([P, T], U16, "word_table1")]
        w1_raw = {}

        def load_words(g):
            nc.sync.dma_start(out=word_table[g][:].bitcast(I32), in_=x_words[g].bitcast(I32))

        def load_w1(g, halves, behind=""):
            width = H // 2 * len(halves)
            raw = sb([P, PACK, width], F32, "w1_raw%d%d" % (g, halves[0]), tag=behind)
            rows = w1[P * PACK * g : P * PACK * (g + 1), H // 2 * halves[0] : H // 2 * halves[0] + width]
            nc.sync.dma_start(out=raw[:], in_=rows.rearrange("(p j) c -> p j c", j=PACK))
            for n, s in enumerate(halves):
                w1_raw[g, s] = raw[:, :, H // 2 * n : H // 2 * (n + 1)]

        offs_sb = load_list("offs_sb", offs)
        nc.sync.dma_start(
            out=scale_table[0:32, :].bitcast(I32), in_=x_scales.bitcast(I32).rearrange("g r c -> r g c")
        )
        load_words(0)
        gate_cols = sb([P, 2, BLOCKS], F32, "gate_cols")
        nc.sync.dma_start(out=gate_cols[:], in_=gate[:, 0, :].rearrange("d (p b) -> p d b", b=BLOCKS))
        load_w1(0, (0,))
        load_w1(1, (0,))
        neighbour_lists = [load_list("pos1_sb", pos1)]
        load_words(1)
        neighbour_lists.append(load_list("pos2_sb", pos2))
        cen_sb = load_list("cen_sb", cen)

        ident = sb([P, P], F32, "ident")
        make_identity(nc, ident[:])

        picked_scales = sb([P, S], U8, "picked_scales")
        nc.vector.tensor_copy(picked_scales[:], scale_table[:].indirect(offs_sb[:]))
        planes = sb([P, PASSES * S], U8, "planes")
        nc.vector.memset(planes[:].bitcast(I32), 0)
        for q in range(QUADRANTS):
            nc.sync.dma_start(
                out=planes[32 * q : 32 * q + 4, :].bitcast(I32).rearrange("p (g c) -> p g c", g=PASSES),
                in_=picked_scales[8 * q : 8 * q + 8, :].bitcast(I32),
            )
        x_scale = [planes[:, S * g : S * (g + 1)] for g in range(PASSES)]
        load_w1(0, (1,), behind=12288)
        load_w1(1, (1,), behind=16384)
        w2_raw = sb([P, PACK, N], F32, "w2_raw", tag="w1_raw10")
        for t in range(PACK):
            nc.sync.dma_start(
                out=w2_raw[:, t, :], in_=w2.rearrange("(q t r) n -> t q r n", t=PACK, r=BLOCK_ROWS)[t]
            )

        x_code = [sb([P, 2 * S], U8, "x_code%d" % g) for g in range(PASSES)]
        w1_code = {}
        w1_scale = {}

        def gather_words(g, half, first, width):
            start = half * BANK + first
            columns = slice(start // LIST_ROWS, (start + width) // LIST_ROWS)
            nc.vector.tensor_copy(
                x_code[g][:, 2 * start : 2 * (start + width)].bitcast(U16), word_table[g][:].indirect(offs_sb[:, columns])
            )

        def round_low(g, s, grouped, copy):
            copy(
                out=grouped.rearrange("p (q c i j) -> p q c j i", c=4, i=4, j=PACK),
                in_=w1_raw[g, s].rearrange("p j (q c i) -> p q c j i", c=8, i=4)[:, :, 0:4],
            )

        def round_high(g, s, grouped, copy, tiles=(0, 1)):
            view = grouped.rearrange("p (e s q c i j) -> p e s q c j i", e=2, s=2, c=2, i=4, j=PACK)
            dealt = w1_raw[g, s].rearrange("p j (q t c i) -> p t q c j i", t=PACK, c=2, i=4)
            for e in tiles:
                copy(out=view[:, e, s], in_=dealt[:, 2 + e])

        def quantize_w1(g, tiles, grouped, behind=""):
            code = sb([P, len(tiles) * P], U32, "w1_code%d%d" % (g, tiles[0]), tag=behind)
            scale = sb([P, len(tiles) * P], U8, "w1_scale%d%d" % (g, tiles[0]))
            nc.vector.quantize_mx(out=code[:].bitcast(FP8X4), scales=scale[:], in_=grouped)
            for e, t in enumerate(tiles):
                w1_code[g, t] = code[:, P * e : P * (e + 1)]
                w1_scale[g, t] = scale[:, P * e : P * (e + 1)]

        wide = P * PACK
        grouped = {
            (g, t): sb([P, n * wide], BF16, "w1_grouped%d%d" % (g, t))
            for g, t, n in ((0, 0, 1), (1, 0, 1), (0, 1, 1), (0, 2, 2), (1, 1, 1), (1, 2, 2))
        }
        gather_words(0, 0, 0, BANK)
        gather_words(0, 1, 0, BANK)
        for g in range(PASSES):
            round_low(g, 0, grouped[g, 0][:], nc.scalar.copy)
            quantize_w1(g, (0,), grouped[g, 0][:])
        round_high(0, 0, grouped[0, 2][:], nc.scalar.copy)
        round_high(1, 0, grouped[1, 2][:], nc.scalar.copy)
        neg_gate = []
        for d in range(2):
            spread = bank(GATE_BANKS[d], "spread%d" % d)
            for b in range(BLOCKS):
                nc.tensor.transpose(
                    spread[:, P * b : P * (b + 1)], gate_cols[:, d, b : b + 1].to_broadcast([P, P]), ident[:]
                )
            neg_gate.append(sb([P, V], F32, "neg_gate%d" % d))
            nc.scalar.activation(
                neg_gate[d][:].rearrange("p (n b) -> p n b", b=BLOCKS),
                spread[:].rearrange("p (b n) -> p n b", b=BLOCKS),
                COPY,
                scale=-1.0,
            )
        for half in range(2):
            for first in (0, BANK // 2):
                gather_words(1, half, first, BANK // 2)
        round_low(0, 1, grouped[0, 1][:], nc.vector.tensor_copy)
        round_high(0, 1, grouped[0, 2][:], nc.vector.tensor_copy, (0,))
        quantize_w1(0, (1,), grouped[0, 1][:])
        round_low(1, 1, grouped[1, 1][:], nc.vector.tensor_copy)
        round_high(0, 1, grouped[0, 2][:], nc.vector.tensor_copy, (1,))
        quantize_w1(1, (1,), grouped[1, 1][:])
        round_high(1, 1, grouped[1, 2][:], nc.vector.tensor_copy)
        quantize_w1(0, (2, 3), grouped[0, 2][:])
        quantize_w1(1, (2, 3), grouped[1, 2][:])

        h = [sb([P, S], F32, "h%d" % t) for t in range(PACK)]

        def first_product(target, g, t, j0, width):
            nc.tensor.matmul_mx(
                out=target,
                lhsT=w1_code[g, t].bitcast(FP8X4),
                lhsT_scale=w1_scale[g, t],
                rhs=x_code[g][:, 2 * j0 : 2 * (j0 + width)].bitcast(FP4X4),
                rhs_scale=x_scale[g][:, j0 : j0 + width],
                start=(g == 0),
                stop=(g == PASSES - 1),
            )

        pieces = ((4, 0, 256), (0, 256, 256), (1, 512, 256), (2, 768, P), (3, 896, P))
        targets = [bank(number, "h_bank0_%d" % number) for number, j0, width in pieces]
        for g in range(PASSES):
            for target, (number, j0, width) in zip(targets, pieces):
                first_product(target[:, 0:width], g, 0, j0, width)
        for target, (number, j0, width) in zip(targets, pieces):
            nc.scalar.copy(h[0][:, j0 : j0 + width], target[:, 0:width])

        def make_h(t):
            targets = [bank(H_BANKS[t] + half, "h_bank%d%d" % (t, half)) for half in range(2)]
            for g in range(PASSES):
                for half in range(2):
                    first_product(targets[half][:], g, t, BANK * half, BANK)
            return targets

        def empty_h(t, targets):
            for half in range(2):
                nc.scalar.copy(h[t][:, BANK * half : BANK * (half + 1)], targets[half][:])

        turned = {}
        rows = {}

        def products(t, v0, width, places=("", "")):
            columns = slice(v0 // LIST_ROWS, (v0 + width) // LIST_ROWS)
            made = []
            for d in range(2):
                made.append(sb([P, width], F32, "product%d_%d_%d" % (d, t, v0), tag=places[d]))
                nc.vector.tensor_tensor(
                    made[d][:], h[t][:].indirect(neighbour_lists[d][:, columns]), neg_gate[d][:, v0 : v0 + width], MULT
                )
            return made

        def centres(t, v0, width, place=""):
            columns = slice(v0 // LIST_ROWS, (v0 + width) // LIST_ROWS)
            made = sb([P, width], F32, "centre%d_%d" % (t, v0), tag=place)
            nc.scalar.activation(made[:], h[t][:].indirect(cen_sb[:, columns]), COPY)
            return [made]

        def add_turned(t, v0, width, terms):
            u, e = divmod(t, 2)
            for b in range(v0 // P, (v0 + width) // P):
                part, place = (e, P * b) if u == 0 else (b // 2, 2 * P * (b % 2) + P * e)
                if (u, part) not in turned:
                    turned[u, part] = bank(TURNED_BANKS[u][part], "turned%d%d" % (u, part))
                for n, term in enumerate(terms):
                    nc.tensor.matmul(
                        turned[u, part][:, place : place + P],
                        lhsT=term[:, P * b - v0 : P * (b + 1) - v0],
                        rhs=ident[:],
                        is_transpose=True,
                        start=(n == 0),
                        stop=(n == len(terms) - 1),
                    )

        rows_low = sb([P, BLOCKS * 2 * P], BF16, "rows_low")
        for b in range(BLOCKS):
            rows[0, b] = rows_low[:, 2 * P * b : 2 * P * (b + 1)]

        def round_low_rows(s):
            nc.scalar.copy(
                out=rows_low[:].rearrange("v (b s q r e) -> v s b q r e", s=2, q=8, r=BLOCK_ROWS, e=2)[:, s],
                in_=turned[0, s][:].rearrange("v (b q e r) -> v b q r e", q=8, r=BLOCK_ROWS, e=2),
            )

        def round_high_rows(pair, blocks):
            made = sb([P, blocks * 2 * P], BF16, "rows_high%d" % pair)
            nc.scalar.copy(
                out=made[:].rearrange("v (b p e) -> v b p e", p=P, e=2),
                in_=turned[1, pair][:, 0 : blocks * 2 * P].rearrange("v (b e p) -> v b p e", p=P, e=2),
            )
            for b in range(blocks):
                rows[1, 2 * pair + b] = made[:, 2 * P * b : 2 * P * (b + 1)]

        def turn_back(back, place, u, b):
            nc.tensor.transpose(back[:, P * place : P * (place + 1)], rows[u, b].bitcast(F32), ident[:])

        def interleave(back, b0, blocks):
            z_grouped = sb([P, blocks * P * PACK], BF16, "z_grouped%d" % b0)
            nc.scalar.copy(
                out=z_grouped[:].bitcast(F32).rearrange("p (b v u) -> p b v u", v=P, u=2),
                in_=back[:, 0 : blocks * 2 * P].rearrange("p (b u v) -> p b v u", v=P, u=2),
            )
            return z_grouped

        def project(piece, blocks, banks):
            width = P * len(blocks)
            z_code = sb([P, width], U32, "z_code%d" % piece)
            z_scale = sb([P, width], U8, "z_scale%d" % piece)
            for n, block in enumerate(blocks):
                cols = slice(P * n, P * (n + 1))
                nc.vector.quantize_mx(out=z_code[:, cols].bitcast(FP8X4), scales=z_scale[:, cols], in_=block)
            for a in range(N // P):
                nc.tensor.matmul_mx(
                    out=banks[a],
                    lhsT=w2_code[:, P * a : P * (a + 1)].bitcast(FP8X4),
                    lhsT_scale=w2_scale[:, P * a : P * (a + 1)],
                    rhs=z_code[:].bitcast(FP8X4),
                    rhs_scale=z_scale[:],
                    start=True,
                    stop=True,
                )

        def store(place, target, copy, name, behind=""):
            result = sb([P, 2 * P], F32, name, tag=behind)
            copy(result[:], place)
            nc.sync.dma_start(out=target, in_=result[:].rearrange("p (a v) -> p a v", a=target.shape[1]))

        terms_0 = products(0, 0, V, ("w1_grouped11", "w1_grouped12")) + centres(0, 0, V)
        empty_h(1, make_h(1))
        empty_h(2, make_h(2))
        banks_3 = make_h(3)
        add_turned(0, 0, V, terms_0)
        terms_1 = products(1, 0, V, (0, 2048)) + centres(1, 0, V, 4096)
        empty_h(3, banks_3)
        add_turned(1, 0, V, terms_1)
        add_turned(2, 0, 2 * P, products(2, 0, 2 * P) + centres(2, 0, 2 * P))
        add_turned(3, 0, 2 * P, products(3, 0, 2 * P) + centres(3, 0, 2 * P, 6144))
        for s in range(2):
            round_low_rows(s)
        round_high_rows(0, 2)
        w2_grouped = []
        for a, place in enumerate((4096, 6144)):
            w2_grouped.append(sb([P, P * PACK], BF16, "w2_grouped%d" % a, tag=place))
            nc.scalar.copy(
                out=w2_grouped[a][:].rearrange("p (c i t) -> p c t i", i=4, t=PACK),
                in_=w2_raw[:, :, P * a : P * (a + 1)].rearrange("p t (c i) -> p c t i", i=4),
            )
        back = bank(BACK_BANKS[0], "back_whole")
        for u in range(2):
            for b in range(2):
                turn_back(back, 2 * b + u, u, b)
        z_0 = [interleave(back[:, 2 * P * b : 2 * P * (b + 1)], b, 1) for b in range(2)]
        back_low = bank(BACK_BANKS[1], "back_low")
        z_late = sb([P, 2 * P * PACK], BF16, "z_late")
        for n in range(2):
            turn_back(back_low, n, 0, 2 + n)
        first = sb([P, 2, P], F32, "centre_last", tag="rows_low")
        for e in range(2):
            nc.scalar.activation(
                first[:, e, :], h[2 + e][:].indirect(cen_sb[:, 3 * P // LIST_ROWS : V // LIST_ROWS]), COPY
            )
        nc.scalar.copy(
            out=z_late[:].bitcast(F32).rearrange("p (v u) -> p v u", u=2)[:, :, 0], in_=back_low[:, 0 : 2 * P]
        )

        second = sb([P, 2, 2 * P], F32, "second", tag=2048)
        for e in range(2):
            nc.vector.tensor_tensor(
                second[:, e, :],
                h[2 + e][:].indirect(neighbour_lists[1][:, 2 * P // LIST_ROWS : V // LIST_ROWS]),
                neg_gate[1][:, 2 * P : V],
                MULT,
            )

        def gather_first(b, behind, sums_behind=""):
            columns = slice(P * b // LIST_ROWS, P * (b + 1) // LIST_ROWS)
            scaled = sb([P, 2, P], F32, "scaled%d" % b, tag=behind)
            first = sb([P, 2, P], F32, "first%d" % b, tag=sums_behind)
            for e in range(2):
                nc.vector.tensor_tensor(
                    scaled[:, e, :],
                    h[2 + e][:].indirect(neighbour_lists[0][:, columns]),
                    neg_gate[0][:, P * b : P * (b + 1)],
                    MULT,
                )
            for e in range(2):
                nc.vector.tensor_tensor(first[:, e, :], h[2 + e][:].indirect(cen_sb[:, columns]), scaled[:, e, :], ADD)
            return first

        def add_late(b, first, other):
            cols = slice(P * (b - 2), P * (b - 1))
            nc.vector.tensor_tensor(
                z_late[:].rearrange("p (v u e) -> p v u e", u=2, e=2)[:, cols, 1, :],
                first[:].rearrange("p e v -> p v e"),
                other.rearrange("p e v -> p v e"),
                ADD,
            )

        first_2 = gather_first(2, 0)
        add_late(2, first_2, second[:, :, 0:P])
        w2_code = sb([P, N], U32, "w2_code")
        w2_scale = sb([P, N], U8, "w2_scale")
        for a in range(N // P):
            cols = slice(P * a, P * (a + 1))
            nc.vector.quantize_mx(out=w2_code[:, cols].bitcast(FP8X4), scales=w2_scale[:, cols], in_=w2_grouped[a][:])
        out_banks = [bank(number, "out_bank%d" % number) for number in OUT_BANKS]
        rows_out = out.rearrange("(a p) v -> p a v", p=P)
        project(0, [block[:] for block in z_0], [out_banks[a][:, 0 : 2 * P] for a in range(2)])
        store(out_banks[0][:, 0 : 2 * P], rows_out[:, 0:1, 0 : 2 * P], nc.scalar.copy, "result0")
        columns = slice(3 * P // LIST_ROWS, V // LIST_ROWS)
        scaled = sb([P, 2, P], F32, "scaled3", tag=1024)
        both = sb([P, 2, P], F32, "both")
        for e in range(2):
            nc.vector.tensor_tensor(
                scaled[:, e, :], h[2 + e][:].indirect(neighbour_lists[0][:, columns]), neg_gate[0][:, 3 * P : V], MULT
            )
        nc.vector.tensor_tensor(both[:], scaled[:], second[:, :, P : 2 * P], ADD)
        add_late(3, first, both[:])
        project(1, [z_late[:, 0 : P * PACK]], [out_banks[2][:, P * a : P * (a + 1)] for a in range(2)])
        store(out_banks[2][:, 0 : 2 * P], rows_out[:, :, 2 * P : 3 * P], nc.scalar.copy, "result2")
        project(2, [z_late[:, P * PACK : 2 * P * PACK]], [out_banks[3][:, P * a : P * (a + 1)] for a in range(2)])
        store(out_banks[1][:, 0 : 2 * P], rows_out[:, 1:2, 0 : 2 * P], nc.vector.tensor_copy, "result1", "both")
        store(out_banks[3][:, 0 : 2 * P], rows_out[:, :, 3 * P : V], nc.vector.tensor_copy, "result3")
